import numpy as np
import ml_dtypes


def mxq(x, axis, fmt="e4m3"):
    dtype, down = {"e4m3": (ml_dtypes.float8_e4m3fn, 7), "e5m2": (ml_dtypes.float8_e5m2, 14)}[fmt]
    v = np.moveaxis(np.asarray(x, np.float32).astype(ml_dtypes.bfloat16).astype(np.float64), axis, -1)
    blocks = v.reshape(v.shape[:-1] + (-1, 32))
    amax = np.abs(blocks).max(-1, keepdims=True)
    byte = np.maximum(np.where(amax > 0, np.frexp(amax)[1] - 1 + 127, 0) - down, 1)
    scale = np.exp2(byte - 127.0)
    codes = (blocks / scale).astype(np.float32).astype(dtype).astype(np.float64)
    return np.moveaxis((codes * scale).reshape(v.shape), -1, axis)


WIDE = False


def mx_kscale(k):
    if not WIDE:
        return np.ones(k)
    levels = np.array([10, -10, 5, -5, 0])
    if k % 512:
        return np.exp2(np.random.permutation(np.resize(levels, k // 32))).repeat(32)
    a = np.empty((k // 512, 16))
    for p in range(k // 512):
        a[p, :8] = np.random.permutation(np.resize(levels, 8))
        for g in range(8):
            far = levels[np.abs(levels - a[p, g]) >= 10]
            a[p, g + 8] = far[np.random.randint(len(far))]
    return np.exp2(a.ravel()).repeat(32)


def f64(x):
    return np.asarray(x).astype(np.float64)


def striped(idx):
    return np.tile(idx.reshape(-1, 16).T, (8, 1)).astype(np.uint16)


def unstriped(offs):
    return offs[:16].T.reshape(-1).astype(np.int64)


def pack_weight(w):
    k, n = w.shape
    w = f64(np.asarray(w, np.float32).astype(ml_dtypes.bfloat16)).reshape(k // 32, 32, n)
    amax = np.abs(w).max(1)
    byte = np.clip(np.where(amax > 0, np.frexp(amax)[1] - 1 + 127 - 7, 1), 1, 254)
    scaled = (w * np.exp2(127.0 - byte)[:, None, :]).reshape(k, n).astype(np.float32)
    words = np.ascontiguousarray(scaled.reshape(k // 512, 128, 4, n).transpose(0, 1, 3, 2)).astype(ml_dtypes.float8_e4m3fn).view(np.uint8)
    return words, np.ascontiguousarray(byte.astype(np.uint8).reshape(k // 512, 16, n))


def unpack_weight(words, scales):
    g, p, n, _ = words.shape
    vals = np.ascontiguousarray(words).view(ml_dtypes.float8_e4m3fn).astype(np.float64) * np.repeat(np.exp2(scales.astype(np.float64) - 127.0), 8, axis=1)[..., None]
    return vals.transpose(0, 1, 3, 2).reshape(g * 512, n)


E2M1 = np.array([0.0, 0.5, 1.0, 1.5, 2.0, 3.0, 4.0, 6.0, -0.0, -0.5, -1.0, -1.5, -2.0, -3.0, -4.0, -6.0])


def pack_fp4(w):
    k, n = w.shape
    w = f64(np.asarray(w, np.float32).astype(ml_dtypes.bfloat16)).reshape(k // 32, 32, n)
    amax = np.abs(w).max(1)
    mant, ex = np.frexp(amax / 6.0)
    byte = np.clip(np.where(amax > 0, np.where(mant > 0.5, ex, ex - 1) + 127, 1), 1, 254)
    scaled = (w * np.exp2(127.0 - byte)[:, None, :]).reshape(k, n).astype(np.float32)
    c = np.ascontiguousarray(scaled.reshape(k // 512, 128, 4, n).transpose(0, 1, 3, 2)).astype(ml_dtypes.float4_e2m1fn).view(np.uint8) & 0xF
    words = (c[..., 0::2] | (c[..., 1::2] << 4)).reshape(k // 512, 128, 2 * n)
    return np.ascontiguousarray(words), np.ascontiguousarray(byte.astype(np.uint8).reshape(k // 512, 16, n))


def unpack_fp4(words, scales):
    g, _, n = scales.shape
    words = np.ascontiguousarray(words).reshape(g, 128, n, 2)
    nib = np.empty((g, 128, n, 4), np.uint8)
    nib[..., 0::2] = words & 0xF
    nib[..., 1::2] = words >> 4
    vals = E2M1[nib] * np.repeat(np.exp2(scales.astype(np.float64) - 127.0), 8, axis=1)[..., None]
    return vals.transpose(0, 1, 3, 2).reshape(g * 512, n)


def relu(v):
    return np.maximum(v, 0.0)


K, T, S, V, H, N = 1024, 1024, 512, 256, 512, 128


def setup_inputs():
    n = np.random.standard_normal
    s = mx_kscale(K)[:, None]
    u = mx_kscale(H)
    near = np.random.permutation(S)
    packed_xT = pack_weight(n((K, T)) * s)
    packed_w2 = pack_fp4(n((H, N)) / np.sqrt(2 * H) / u[:, None])
    packed_w3 = pack_fp4(n((H, N)) / np.sqrt(2 * H) / u[:, None])
    return {
        "x_words": packed_xT[0],
        "x_scales": packed_xT[1],
        "w1": (n((K, H)) / np.sqrt(K) / s * u).astype(np.float32),
        "w2_words": packed_w2[0],
        "w2_scales": packed_w2[1],
        "w3_words": packed_w3[0],
        "w3_scales": packed_w3[1],
        "offs": striped(np.random.permutation(T)[:S]),
        "pos1": striped(near[:V]),
        "pos2": striped(near[V:]),
        "pos3": striped(np.random.permutation(S)[:V]),
        "foe1": striped(np.random.permutation(S)[:V]),
        "foe2": striped(np.random.permutation(S)[:V]),
        "foe3": striped(np.random.permutation(S)[:V]),
    }


def reference(x_words, x_scales, w1, w2_words, w2_scales, w3_words, w3_scales, offs, pos1, pos2, pos3, foe1, foe2, foe3):
    xq = unpack_weight(x_words, x_scales)[:, unstriped(offs)]
    h = relu(mxq(f64(w1), 0, "e4m3").T @ xq)
    zp = (h[:, unstriped(pos1)] + h[:, unstriped(pos2)] + h[:, unstriped(pos3)]) / 3
    zn = (h[:, unstriped(foe1)] + h[:, unstriped(foe2)] + h[:, unstriped(foe3)]) / 3
    return np.tanh(unpack_fp4(w2_words, w2_scales).T @ mxq(zp, 0, "e4m3") + unpack_fp4(w3_words, w3_scales).T @ mxq(zn, 0, "e4m3"))

@@ -1,0 +1,230 @@
+from contextlib import ExitStack
+
+import concourse.mybir as mybir
+from concourse.masks import make_identity
+
+K, T, S, V, H, N = 1024, 1024, 512, 256, 512, 128
+FLOPS = 2 * K * H * S + 2 * 2 * H * N * V
+
+F32 = mybir.dt.float32
+BF16 = mybir.dt.bfloat16
+I32 = mybir.dt.int32
+U32 = mybir.dt.uint32
+U16 = mybir.dt.uint16
+U8 = mybir.dt.uint8
+FP8X4 = mybir.dt.float8_e4m3fn_x4
+FP4X4 = mybir.dt.float4_e2m1fn_x4
+ACT = mybir.ActivationFunctionType
+ALU = mybir.AluOpType
+
+P = 128
+PACK = 4
+K_PASS = P * PACK
+PASSES = K // K_PASS
+TILES = H // P
+HALVES = V // P
+DEGREE = 3
+
+
+def tile_picked_zsgn_mean_p_kernel(
+    tc, x_words, x_scales, w1, w2_words, w2_scales, w3_words, w3_scales, offs, pos1, pos2, pos3, foe1, foe2, foe3, out
+):
+    nc = tc.nc
+    with ExitStack() as ctx:
+        keep = ctx.enter_context(tc.tile_pool(name="keep", bufs=1))
+        psum = ctx.enter_context(tc.psum_pool(name="psum", bufs=1))
+
+        def load_list(src, name):
+            tile = keep.tile(list(src.shape), U16, name=name)
+            nc.sync.dma_start(tile[:], src)
+            return tile
+
+        def load_words(o):
+            tile = keep.tile([P, T], U32, name=f"x_window{o}", align_bytes=64)
+            nc.sync.dma_start(tile[:].bitcast(I32), x_words[o].rearrange("p n t -> p (n t)").bitcast(I32))
+            return tile
+
+        def load_w1(o, first_tile, tiles):
+            tile = keep.tile([P, PACK, tiles * P], F32, name=f"w1_raw{o}_{first_tile}", align_bytes=64)
+            rows = w1[o * K_PASS : (o + 1) * K_PASS, first_tile * P : (first_tile + tiles) * P]
+            nc.sync.dma_start(tile[:], rows.rearrange("(p j) c -> p j c", j=PACK))
+            return [tile[:, :, i * P : (i + 1) * P] for i in range(tiles)]
+
+        scale_window = keep.tile([P, T], U8, name="scale_window", align_bytes=64)
+        nc.gpsimd.memset(scale_window[:].bitcast(I32), 0)
+        w_scales = keep.tile([P, 2 * N], U8, name="w_scales", align_bytes=64)
+        nc.vector.memset(w_scales[:].bitcast(I32), 0)
+        ident = keep.tile([P, P], F32, name="ident", align_bytes=64)
+        make_identity(nc, ident[:])
+
+        x_window = [load_words(0)]
+        picked = load_list(offs, "offs")
+        for q in range(4):
+            rows = slice(32 * q, 32 * q + 4 * PASSES)
+            nc.scalar.dma_start(scale_window[rows, :].bitcast(I32), x_scales[:, 4 * q : 4 * q + 4, :].bitcast(I32))
+        x_window.append(load_words(1))
+        w1_raw = {}
+        for o in range(PASSES):
+            (w1_raw[0, o],) = load_w1(o, 0, 1)
+        friends = [load_list(src, name) for src, name in ((pos1, "pos1"), (pos2, "pos2"), (pos3, "pos3"))]
+        for o in range(PASSES):
+            (w1_raw[1, o],) = load_w1(o, 1, 1)
+        foes = [load_list(src, name) for src, name in ((foe1, "foe1"), (foe2, "foe2"), (foe3, "foe3"))]
+        for o in range(PASSES):
+            w1_raw[2, o], w1_raw[3, o] = load_w1(o, 2, 2)
+        w_words = []
+        for z, (words, scales) in enumerate(((w2_words, w2_scales), (w3_words, w3_scales))):
+            tile = keep.tile([P, 2 * N], U8, name=f"w_words{z}", align_bytes=64)
+            nc.sync.dma_start(tile[:].bitcast(I32), words[0].bitcast(I32))
+            w_words.append(tile)
+            for q in range(4):
+                nc.sync.dma_start(
+                    w_scales[32 * q : 32 * q + 4, z * N : (z + 1) * N].bitcast(I32),
+                    scales[0, 4 * q : 4 * q + 4, :].bitcast(I32),
+                )
+        lists = [friends, foes]
+
+        x_all = []
+        for o in range(PASSES):
+            tile = keep.tile([P, S], U32, name=f"x_codes{o}", align_bytes=64)
+            nc.vector.tensor_copy(tile[:], x_window[o][:].indirect(picked[:]))
+            x_all.append(tile)
+
+        w1_codes, w1_scale = {}, {}
+
+        def quantise_w1(t, o):
+            grouped = keep.tile([P, P, PACK], BF16, name=f"w1_grouped{t}_{o}", tag=f"stage{t}_{o}", align_bytes=64)
+            nc.scalar.copy(
+                grouped[:].rearrange("p (c i) j -> p c j i", i=4), w1_raw[t, o].rearrange("p j (c i) -> p c j i", i=4)
+            )
+            w1_codes[t, o] = keep.tile([P, P], U32, name=f"w1_codes{t}_{o}", align_bytes=64)
+            w1_scale[t, o] = keep.tile([P, P], U8, name=f"w1_scale{t}_{o}", align_bytes=64)
+            nc.vector.quantize_mx(
+                out=w1_codes[t, o][:].bitcast(FP8X4), scales=w1_scale[t, o][:], in_=grouped[:].rearrange("p c j -> p (c j)")
+            )
+
+        for o in range(PASSES):
+            quantise_w1(0, o)
+        pieces = ((0, 256), (256, 128), (384, 128))
+        x_scale = keep.tile([P, S], U8, name="x_scale", align_bytes=64)
+        for first, width in pieces:
+            nc.vector.tensor_copy(
+                x_scale[:, first : first + width], scale_window[:].indirect(picked[:, first // 16 : (first + width) // 16])
+            )
+
+        h = [keep.tile([P, S], F32, name=f"h{t}", align_bytes=64) for t in range(TILES)]
+
+        def hidden(t, first, width, tag):
+            acc = psum.tile([P, width], F32, name=tag, tag=tag)
+            cols = slice(first, first + width)
+            for o in range(PASSES):
+                nc.tensor.matmul_mx(
+                    out=acc[:],
+                    lhsT=w1_codes[t, o][:].bitcast(FP8X4),
+                    lhsT_scale=w1_scale[t, o][:],
+                    rhs=x_all[o][:, cols].bitcast(FP8X4),
+                    rhs_scale=x_scale[4 * o : P, cols],
+                    start=(o == 0),
+                    stop=(o == PASSES - 1),
+                )
+            nc.scalar.activation(h[t][:, cols], acc[:], ACT.Relu)
+
+        for (first, width), tag in zip(pieces, ("bank0", "bank1", "bank7")):
+            hidden(0, first, width, tag)
+        for t in range(1, TILES):
+            for o in range(PASSES):
+                quantise_w1(t, o)
+            hidden(t, 0, S, ("bank6", "bank0", "bank1")[t - 1])
+
+        sum_tags = [["bank2", "bank3"], ["bank4", "bank5"]]
+        sums = [[psum.tile([P, H], F32, name=f"sum{z}_{b}", tag=sum_tags[z][b]) for b in range(HALVES)] for z in range(2)]
+        last_sums = [None] * HALVES
+        mean_t = [[keep.tile([P, H], BF16, name=f"mean_t{z}_{b}", align_bytes=64) for b in range(HALVES)] for z in range(2)]
+
+        def neighbours(z, t, split_last):
+            tag = {(1, 0): "stage1_1", (0, 1): "stage2_1", (1, 1): "stage3_1"}.get((z, t), f"got{z}_{t}")
+            got_all = keep.tile([P, DEGREE, V], F32, name=f"got{z}_{t}", tag=tag, align_bytes=64)
+            banks = sums[z]
+            if split_last:
+                for b in range(HALVES):
+                    last_sums[b] = psum.tile([P, H], F32, name=f"last_sum{b}", tag=sum_tags[0][b])
+                banks = last_sums
+            for d in range(DEGREE):
+                got = got_all[:, d, :]
+                if split_last and d == DEGREE - 1:
+                    for b in range(HALVES):
+                        nc.vector.tensor_copy(
+                            got[:, b * P : (b + 1) * P], h[t][:].indirect(lists[z][d][:, b * P // 16 : (b + 1) * P // 16])
+                        )
+                else:
+                    nc.vector.tensor_copy(got, h[t][:].indirect(lists[z][d][:]))
+                for b in range(HALVES):
+                    nc.tensor.matmul(
+                        banks[b][:, t * P : (t + 1) * P],
+                        lhsT=got[:, b * P : (b + 1) * P],
+                        rhs=ident[:],
+                        is_transpose=True,
+                        start=(d == 0),
+                        stop=(d == DEGREE - 1),
+                    )
+
+        def round_mean(z, b, bank, first_tile, tiles, on_vector):
+            words = slice(first_tile * P // PACK, (first_tile + tiles) * P // PACK)
+            dst = mean_t[z][b][:].rearrange("v (u p e) -> v u p e", u=2, e=2)[:, :, words, :]
+            src = bank[:].rearrange("v (p u e) -> v u p e", u=2, e=2)[:, :, words, :]
+            if on_vector:
+                nc.vector.tensor_scalar(dst, src, 1.0 / DEGREE, None, ALU.mult)
+            else:
+                nc.scalar.activation(dst, src, ACT.Copy, scale=1.0 / DEGREE)
+
+        z_codes, z_scale = {}, {}
+
+        def quantise_mean(z, b, on_vector):
+            back = psum.tile([P, 2, P], F32, name=f"back{z}_{b}", tag=f"bank{6 + b}")
+            pairs = mean_t[z][b][:].bitcast(F32)
+            for u in range(2):
+                nc.tensor.transpose(back[:, u, :], pairs[:, u * P : (u + 1) * P], ident[:])
+            grouped = keep.tile([P, P * PACK], BF16, name=f"z_grouped{z}_{b}", align_bytes=64)
+            dst = grouped[:].bitcast(F32).rearrange("p (v u) -> p v u", u=2)
+            src = back[:].rearrange("p u v -> p v u")
+            if on_vector:
+                nc.vector.tensor_copy(dst, src)
+            else:
+                nc.scalar.copy(dst, src)
+            z_codes[z, b] = keep.tile([P, P], U32, name=f"z_codes{z}_{b}", align_bytes=64)
+            z_scale[z, b] = keep.tile([P, P], U8, name=f"z_scale{z}_{b}", align_bytes=64)
+            nc.vector.quantize_mx(out=z_codes[z, b][:].bitcast(FP8X4), scales=z_scale[z, b][:], in_=grouped[:])
+
+        acc_out = {}
+
+        def product(z, b):
+            if z == 0:
+                acc_out[b] = psum.tile([P, P], F32, name=f"acc_out{b}", tag=f"bank{b}")
+            nc.tensor.matmul_mx(
+                out=acc_out[b][:],
+                lhsT=w_words[z][:].bitcast(FP4X4),
+                lhsT_scale=w_scales[:, z * N : (z + 1) * N],
+                rhs=z_codes[z, b][:].bitcast(FP8X4),
+                rhs_scale=z_scale[z, b][:],
+                start=(z == 0),
+                stop=(z == 1),
+            )
+
+        for z, t in ((0, 0), (1, 0), (0, 1), (1, 1), (0, 2), (0, 3)):
+            neighbours(z, t, False)
+        for b in range(HALVES):
+            round_mean(0, b, sums[0][b], 0, TILES, False)
+        for b in range(HALVES):
+            quantise_mean(0, b, False)
+            product(0, b)
+        neighbours(1, 2, False)
+        for b in range(HALVES):
+            round_mean(1, b, sums[1][b], 0, TILES - 1, False)
+        neighbours(1, 3, True)
+        for b in range(HALVES):
+            round_mean(1, b, last_sums[b], TILES - 1, 1, b == 0)
+            quantise_mean(1, b, b == 0)
+            product(1, b)
+            result = keep.tile([P, P], F32, name=f"result{b}", align_bytes=64)
+            nc.scalar.activation(result[:], acc_out[b][:], ACT.Tanh)
+            nc.sync.dma_start(out[:, b * P : (b + 1) * P], result[:])

@@ -24,6 +24,9 @@ PASSES = K // K_PASS
 TILES = H // P
 HALVES = V // P
 DEGREE = 3
+CHUNK_STEP, CHUNK_WORDS = 42, 44
+TURNED = PACK - 1
+ALIGN = 8
 
 
 def tile_picked_zsgn_mean_p_kernel(
@@ -44,11 +47,12 @@ def tile_picked_zsgn_mean_p_kernel(
             nc.sync.dma_start(tile[:].bitcast(I32), x_words[o].rearrange("p n t -> p (n t)").bitcast(I32))
             return tile
 
-        def load_w1(o, first_tile, tiles):
-            tile = keep.tile([P, PACK, tiles * P], F32, name=f"w1_raw{o}_{first_tile}", align_bytes=64)
-            rows = w1[o * K_PASS : (o + 1) * K_PASS, first_tile * P : (first_tile + tiles) * P]
+        def load_w1(c, o):
+            tile = keep.tile([P, PACK, CHUNK_WORDS * PACK], F32, name=f"w1_raw{c}_{o}", align_bytes=64)
+            first = c * CHUNK_STEP * PACK
+            rows = w1[o * K_PASS : (o + 1) * K_PASS, first : first + CHUNK_WORDS * PACK]
             nc.sync.dma_start(tile[:], rows.rearrange("(p j) c -> p j c", j=PACK))
-            return [tile[:, :, i * P : (i + 1) * P] for i in range(tiles)]
+            return tile[:].rearrange("p j (m i) -> p m j i", i=PACK)
 
         scale_window = keep.tile([P, T], U8, name="scale_window", align_bytes=64)
         nc.gpsimd.memset(scale_window[:].bitcast(I32), 0)
@@ -57,21 +61,21 @@ def tile_picked_zsgn_mean_p_kernel(
         ident = keep.tile([P, P], F32, name="ident", align_bytes=64)
         make_identity(nc, ident[:])
 
-        x_window = [load_words(0)]
         picked = load_list(offs, "offs")
+        x_window = [load_words(0)]
         for q in range(4):
             rows = slice(32 * q, 32 * q + 4 * PASSES)
-            nc.scalar.dma_start(scale_window[rows, :].bitcast(I32), x_scales[:, 4 * q : 4 * q + 4, :].bitcast(I32))
-        x_window.append(load_words(1))
+            nc.sync.dma_start(scale_window[rows, :].bitcast(I32), x_scales[:, 4 * q : 4 * q + 4, :].bitcast(I32))
         w1_raw = {}
         for o in range(PASSES):
-            (w1_raw[0, o],) = load_w1(o, 0, 1)
+            w1_raw[0, o] = load_w1(0, o)
+        x_window.append(load_words(1))
         friends = [load_list(src, name) for src, name in ((pos1, "pos1"), (pos2, "pos2"), (pos3, "pos3"))]
         for o in range(PASSES):
-            (w1_raw[1, o],) = load_w1(o, 1, 1)
+            w1_raw[1, o] = load_w1(1, o)
         foes = [load_list(src, name) for src, name in ((foe1, "foe1"), (foe2, "foe2"), (foe3, "foe3"))]
         for o in range(PASSES):
-            w1_raw[2, o], w1_raw[3, o] = load_w1(o, 2, 2)
+            w1_raw[2, o] = load_w1(2, o)
         w_words = []
         for z, (words, scales) in enumerate(((w2_words, w2_scales), (w3_words, w3_scales))):
             tile = keep.tile([P, 2 * N], U8, name=f"w_words{z}", align_bytes=64)
@@ -84,32 +88,44 @@ def tile_picked_zsgn_mean_p_kernel(
                 )
         lists = [friends, foes]
 
-        x_all = []
-        for o in range(PASSES):
-            tile = keep.tile([P, S], U32, name=f"x_codes{o}", align_bytes=64)
-            nc.vector.tensor_copy(tile[:], x_window[o][:].indirect(picked[:]))
-            x_all.append(tile)
+        x_all = [keep.tile([P, S], U32, name="x_codes0", align_bytes=64)]
+        nc.vector.tensor_copy(x_all[0][:], x_window[0][:].indirect(picked[:]))
+        x_scale = keep.tile([P, S], U8, name="x_scale", align_bytes=64)
+        nc.vector.tensor_copy(x_scale[:], scale_window[:].indirect(picked[:]))
 
         w1_codes, w1_scale = {}, {}
 
         def quantise_w1(t, o):
-            grouped = keep.tile([P, P, PACK], BF16, name=f"w1_grouped{t}_{o}", tag=f"stage{t}_{o}", align_bytes=64)
-            nc.scalar.copy(
-                grouped[:].rearrange("p (c i) j -> p c j i", i=4), w1_raw[t, o].rearrange("p j (c i) -> p c j i", i=4)
+            stage = keep.tile([P, P + 2 * ALIGN, PACK], BF16, name=f"w1_grouped{t}_{o}", tag=f"stage{t}_{o}", align_bytes=64)
+            grouped = stage[:, ALIGN : ALIGN + P, :]
+            if t < TURNED:
+                lead = t * P - TURNED * CHUNK_STEP * t
+                m0, m1 = lead // TURNED, (lead + P - 1) // TURNED + 1
+                first = ALIGN - (lead - TURNED * m0)
+                dst = stage[:, first : first + TURNED * (m1 - m0), :].rearrange("p (m i) j -> p m j i", i=TURNED)
+                nc.scalar.copy(dst, w1_raw[t, o][:, m0:m1, :, 0:TURNED])
+            else:
+                done = 0
+                for c in range(TURNED):
+                    m0 = done - c * CHUNK_STEP
+                    count = CHUNK_WORDS - m0
+                    nc.scalar.copy(grouped[:, done : done + count, :], w1_raw[c, o][:, m0:CHUNK_WORDS, :, TURNED])
+                    done += count
+            w1_codes[t, o] = keep.tile(
+                [P, P], U32, name=f"w1_codes{t}_{o}", tag="stage1_1" if (t, o) == (0, 1) else f"w1_codes{t}_{o}", align_bytes=64
             )
-            w1_codes[t, o] = keep.tile([P, P], U32, name=f"w1_codes{t}_{o}", align_bytes=64)
             w1_scale[t, o] = keep.tile([P, P], U8, name=f"w1_scale{t}_{o}", align_bytes=64)
             nc.vector.quantize_mx(
-                out=w1_codes[t, o][:].bitcast(FP8X4), scales=w1_scale[t, o][:], in_=grouped[:].rearrange("p c j -> p (c j)")
+                out=w1_codes[t, o][:].bitcast(FP8X4), scales=w1_scale[t, o][:], in_=grouped.rearrange("p c j -> p (c j)")
             )
 
         for o in range(PASSES):
             quantise_w1(0, o)
         pieces = ((0, 256), (256, 128), (384, 128))
-        x_scale = keep.tile([P, S], U8, name="x_scale", align_bytes=64)
+        x_all.append(keep.tile([P, S], U32, name="x_codes1", tag="stage0_1", align_bytes=64))
         for first, width in pieces:
             nc.vector.tensor_copy(
-                x_scale[:, first : first + width], scale_window[:].indirect(picked[:, first // 16 : (first + width) // 16])
+                x_all[1][:, first : first + width], x_window[1][:].indirect(picked[:, first // 16 : (first + width) // 16])
             )
 
         h = [keep.tile([P, S], F32, name=f"h{t}", align_bytes=64) for t in range(TILES)]
@@ -136,72 +152,47 @@ def tile_picked_zsgn_mean_p_kernel(
                 quantise_w1(t, o)
             hidden(t, 0, S, ("bank6", "bank0", "bank1")[t - 1])
 
-        sum_tags = [["bank2", "bank3"], ["bank4", "bank5"]]
-        sums = [[psum.tile([P, H], F32, name=f"sum{z}_{b}", tag=sum_tags[z][b]) for b in range(HALVES)] for z in range(2)]
-        last_sums = [None] * HALVES
-        mean_t = [[keep.tile([P, H], BF16, name=f"mean_t{z}_{b}", align_bytes=64) for b in range(HALVES)] for z in range(2)]
+        mean_t = [[keep.tile([P, 2, P, 2], BF16, name=f"mean_t{z}_{b}", align_bytes=64) for b in range(HALVES)] for z in range(2)]
 
-        def neighbours(z, t, split_last):
-            tag = {(1, 0): "stage1_1", (0, 1): "stage2_1", (1, 1): "stage3_1"}.get((z, t), f"got{z}_{t}")
-            got_all = keep.tile([P, DEGREE, V], F32, name=f"got{z}_{t}", tag=tag, align_bytes=64)
-            banks = sums[z]
-            if split_last:
-                for b in range(HALVES):
-                    last_sums[b] = psum.tile([P, H], F32, name=f"last_sum{b}", tag=sum_tags[0][b])
-                banks = last_sums
-            for d in range(DEGREE):
-                got = got_all[:, d, :]
-                if split_last and d == DEGREE - 1:
-                    for b in range(HALVES):
-                        nc.vector.tensor_copy(
-                            got[:, b * P : (b + 1) * P], h[t][:].indirect(lists[z][d][:, b * P // 16 : (b + 1) * P // 16])
-                        )
-                else:
+        def turned_sums(z, t, banks, first, groups):
+            for ds, tag in groups:
+                got_all = keep.tile([P, len(ds), V], F32, name=f"got{z}_{t}_{ds[0]}", tag=tag or f"got{z}_{t}_{ds[0]}", align_bytes=64)
+                for i, d in enumerate(ds):
+                    got = got_all[:, i, :]
                     nc.vector.tensor_copy(got, h[t][:].indirect(lists[z][d][:]))
-                for b in range(HALVES):
-                    nc.tensor.matmul(
-                        banks[b][:, t * P : (t + 1) * P],
-                        lhsT=got[:, b * P : (b + 1) * P],
-                        rhs=ident[:],
-                        is_transpose=True,
-                        start=(d == 0),
-                        stop=(d == DEGREE - 1),
-                    )
+                    for b in range(HALVES):
+                        nc.tensor.matmul(
+                            banks[b][:, first : first + P],
+                            lhsT=got[:, b * P : (b + 1) * P],
+                            rhs=ident[:],
+                            is_transpose=True,
+                            start=(d == 0),
+                            stop=(d == DEGREE - 1),
+                        )
 
-        def round_mean(z, b, bank, first_tile, tiles, on_vector):
-            words = slice(first_tile * P // PACK, (first_tile + tiles) * P // PACK)
-            dst = mean_t[z][b][:].rearrange("v (u p e) -> v u p e", u=2, e=2)[:, :, words, :]
-            src = bank[:].rearrange("v (p u e) -> v u p e", u=2, e=2)[:, :, words, :]
-            if on_vector:
-                nc.vector.tensor_scalar(dst, src, 1.0 / DEGREE, None, ALU.mult)
-            else:
-                nc.scalar.activation(dst, src, ACT.Copy, scale=1.0 / DEGREE)
+        def round_turned(z, b, bank):
+            src = bank[:].rearrange("v (p j) -> v p j", j=TURNED)
+            nc.scalar.activation(mean_t[z][b][:, 0, :, :], src[:, :, 0:2], ACT.Copy, scale=1.0 / DEGREE)
+            nc.scalar.activation(mean_t[z][b][:, 1, :, :], src[:, :, 2:3].to_broadcast([P, P, 2]), ACT.Copy, scale=1.0 / DEGREE)
 
-        z_codes, z_scale = {}, {}
+        z_grouped, z_codes, z_scale = {}, {}, {}
 
-        def quantise_mean(z, b, on_vector):
-            back = psum.tile([P, 2, P], F32, name=f"back{z}_{b}", tag=f"bank{6 + b}")
-            pairs = mean_t[z][b][:].bitcast(F32)
+        def turn_back(z, b, tag):
+            back = psum.tile([P, 2, P], F32, name=f"back{z}_{b}", tag=tag)
+            pairs = mean_t[z][b][:].rearrange("v u p e -> v (u p e)").bitcast(F32)
             for u in range(2):
                 nc.tensor.transpose(back[:, u, :], pairs[:, u * P : (u + 1) * P], ident[:])
-            grouped = keep.tile([P, P * PACK], BF16, name=f"z_grouped{z}_{b}", align_bytes=64)
-            dst = grouped[:].bitcast(F32).rearrange("p (v u) -> p v u", u=2)
-            src = back[:].rearrange("p u v -> p v u")
-            if on_vector:
-                nc.vector.tensor_copy(dst, src)
-            else:
-                nc.scalar.copy(dst, src)
+            z_grouped[z, b] = keep.tile([P, P * PACK], BF16, name=f"z_grouped{z}_{b}", align_bytes=64)
+            nc.scalar.copy(z_grouped[z, b][:].bitcast(F32).rearrange("p (v u) -> p v u", u=2), back[:].rearrange("p u v -> p v u"))
+
+        def quantise_mean(z, b):
             z_codes[z, b] = keep.tile([P, P], U32, name=f"z_codes{z}_{b}", align_bytes=64)
             z_scale[z, b] = keep.tile([P, P], U8, name=f"z_scale{z}_{b}", align_bytes=64)
-            nc.vector.quantize_mx(out=z_codes[z, b][:].bitcast(FP8X4), scales=z_scale[z, b][:], in_=grouped[:])
+            nc.vector.quantize_mx(out=z_codes[z, b][:].bitcast(FP8X4), scales=z_scale[z, b][:], in_=z_grouped[z, b][:])
 
-        acc_out = {}
-
-        def product(z, b):
-            if z == 0:
-                acc_out[b] = psum.tile([P, P], F32, name=f"acc_out{b}", tag=f"bank{b}")
+        def product(z, b, acc):
             nc.tensor.matmul_mx(
-                out=acc_out[b][:],
+                out=acc[:],
                 lhsT=w_words[z][:].bitcast(FP4X4),
                 lhsT_scale=w_scales[:, z * N : (z + 1) * N],
                 rhs=z_codes[z, b][:].bitcast(FP8X4),
@@ -210,21 +201,46 @@ def tile_picked_zsgn_mean_p_kernel(
                 stop=(z == 1),
             )
 
-        for z, t in ((0, 0), (1, 0), (0, 1), (1, 1), (0, 2), (0, 3)):
-            neighbours(z, t, False)
+        sums = [
+            [psum.tile([P, TURNED * P], F32, name=f"sum{z}_{b}", tag=f"bank{2 + 2 * z + b}") for b in range(HALVES)]
+            for z in range(2)
+        ]
+        turned_sums(0, 0, sums[0], 0, (((0,), None), ((1, 2), "stage1_0")))
+        turned_sums(1, 0, sums[1], 0, (((0, 1, 2), "stage1_1"),))
+        turned_sums(0, 1, sums[0], P, (((0,), None), ((1, 2), "stage2_0")))
+        turned_sums(1, 1, sums[1], P, (((0, 1, 2), "stage2_1"),))
+        turned_sums(1, 2, sums[1], 2 * P, (((0,), None), ((1, 2), "stage3_0")))
         for b in range(HALVES):
-            round_mean(0, b, sums[0][b], 0, TILES, False)
+            round_turned(1, b, sums[1][b])
+            turn_back(1, b, f"bank{b}")
+        turned_sums(0, 2, sums[0], 2 * P, (((0, 1, 2), "stage3_1"),))
         for b in range(HALVES):
-            quantise_mean(0, b, False)
-            product(0, b)
-        neighbours(1, 2, False)
+            round_turned(0, b, sums[0][b])
+        last = [psum.tile([P, P], F32, name=f"last{b}", tag=f"bank{6 + b}") for b in range(HALVES)]
+        turned_sums(0, 3, last, 0, (((0, 1, 2), None),))
         for b in range(HALVES):
-            round_mean(1, b, sums[1][b], 0, TILES - 1, False)
-        neighbours(1, 3, True)
+            nc.scalar.activation(mean_t[0][b][:, 1, :, 1], last[b][:], ACT.Copy, scale=1.0 / DEGREE)
+            turn_back(0, b, f"bank{4 + b}")
+
+        part = [keep.tile([P, V], F32, name=f"part{d}", align_bytes=64) for d in range(DEGREE)]
+        for d in range(DEGREE):
+            for b in range(HALVES):
+                cols = slice(b * P, (b + 1) * P)
+                window = h[TURNED][:].indirect(foes[d][:, b * P // 16 : (b + 1) * P // 16])
+                if d == 0:
+                    nc.vector.tensor_copy(part[d][:, cols], window)
+                else:
+                    nc.vector.tensor_tensor(part[d][:, cols], window, part[d - 1][:, cols], ALU.add)
         for b in range(HALVES):
-            round_mean(1, b, last_sums[b], TILES - 1, 1, b == 0)
-            quantise_mean(1, b, b == 0)
-            product(1, b)
+            plane = z_grouped[1, b][:].rearrange("p (v j) -> p v j", j=PACK)[:, :, TURNED]
+            nc.vector.tensor_scalar(plane, part[DEGREE - 1][:, b * P : (b + 1) * P], 1.0 / DEGREE, None, ALU.mult)
+        acc = [psum.tile([P, P], F32, name=f"acc_out{b}", tag=f"bank{2 + b}") for b in range(HALVES)]
+        for b in range(HALVES):
+            quantise_mean(0, b)
+            product(0, b, acc[b])
+        for b in range(HALVES):
+            quantise_mean(1, b)
+            product(1, b, acc[b])
             result = keep.tile([P, P], F32, name=f"result{b}", align_bytes=64)
-            nc.scalar.activation(result[:], acc_out[b][:], ACT.Tanh)
+            nc.scalar.activation(result[:], acc[b][:], ACT.Tanh)
             nc.sync.dma_start(out[:, b * P : (b + 1) * P], result[:])

@@ -114,7 +114,9 @@ def tile_picked_zsgn_mean_p_kernel(
             w1_codes[t, o] = keep.tile(
                 [P, P], U32, name=f"w1_codes{t}_{o}", tag="stage1_1" if (t, o) == (0, 1) else f"w1_codes{t}_{o}", align_bytes=64
             )
-            w1_scale[t, o] = keep.tile([P, P], U8, name=f"w1_scale{t}_{o}", align_bytes=64)
+            w1_scale[t, o] = keep.tile(
+                [P, P], U8, name=f"w1_scale{t}_{o}", tag="stage1_0" if (t, o) == (0, 1) else f"w1_scale{t}_{o}", align_bytes=64
+            )
             nc.vector.quantize_mx(
                 out=w1_codes[t, o][:].bitcast(FP8X4), scales=w1_scale[t, o][:], in_=grouped.rearrange("p c j -> p (c j)")
             )
@@ -205,7 +207,7 @@ def tile_picked_zsgn_mean_p_kernel(
             [psum.tile([P, TURNED * P], F32, name=f"sum{z}_{b}", tag=f"bank{2 + 2 * z + b}") for b in range(HALVES)]
             for z in range(2)
         ]
-        turned_sums(0, 0, sums[0], 0, (((0,), None), ((1, 2), "stage1_0")))
+        turned_sums(0, 0, sums[0], 0, (((0, 1), None), ((2,), "stage1_0")))
         turned_sums(1, 0, sums[1], 0, (((0, 1, 2), "stage1_1"),))
         turned_sums(0, 1, sums[0], P, (((0,), None), ((1, 2), "stage2_0")))
         turned_sums(1, 1, sums[1], P, (((0, 1, 2), "stage2_1"),))
@@ -243,4 +245,4 @@ def tile_picked_zsgn_mean_p_kernel(
             product(1, b, acc[b])
             result = keep.tile([P, P], F32, name=f"result{b}", align_bytes=64)
             nc.scalar.activation(result[:], acc[b][:], ACT.Tanh)
-            nc.sync.dma_start(out[:, b * P : (b + 1) * P], result[:])
+            (nc.sync, nc.scalar)[b].dma_start(out[:, b * P : (b + 1) * P], result[:])

@@ -27,6 +27,7 @@ DEGREE = 3
 CHUNK_STEP, CHUNK_WORDS = 42, 44
 TURNED = PACK - 1
 ALIGN = 8
+SCALAR_WORDS = 21
 
 
 def tile_picked_zsgn_mean_p_kernel(
@@ -103,7 +104,12 @@ def tile_picked_zsgn_mean_p_kernel(
                 m0, m1 = lead // TURNED, (lead + P - 1) // TURNED + 1
                 first = ALIGN - (lead - TURNED * m0)
                 dst = stage[:, first : first + TURNED * (m1 - m0), :].rearrange("p (m i) j -> p m j i", i=TURNED)
-                nc.scalar.copy(dst, w1_raw[t, o][:, m0:m1, :, 0:TURNED])
+                src = w1_raw[t, o][:, m0:m1, :, 0:TURNED]
+                if (t, o) == (0, 1):
+                    nc.scalar.copy(dst[:, :SCALAR_WORDS], src[:, :SCALAR_WORDS])
+                    nc.vector.tensor_copy(dst[:, SCALAR_WORDS:], src[:, SCALAR_WORDS:])
+                else:
+                    nc.scalar.copy(dst, src)
             else:
                 done = 0
                 for c in range(TURNED):
@@ -152,7 +158,11 @@ def tile_picked_zsgn_mean_p_kernel(
         for t in range(1, TILES):
             for o in range(PASSES):
                 quantise_w1(t, o)
-            hidden(t, 0, S, ("bank6", "bank0", "bank1")[t - 1])
+            if t == 1:
+                for s in range(2):
+                    hidden(t, s * S // 2, S // 2, f"bank{6 + s}")
+            else:
+                hidden(t, 0, S, f"bank{t - 2}")
 
         mean_t = [[keep.tile([P, 2, P, 2], BF16, name=f"mean_t{z}_{b}", align_bytes=64) for b in range(HALVES)] for z in range(2)]
 

@@ -36,6 +36,7 @@ def tile_picked_zsgn_mean_p_kernel(
     nc = tc.nc
     with ExitStack() as ctx:
         keep = ctx.enter_context(tc.tile_pool(name="keep", bufs=1))
+        shared = ctx.enter_context(tc.tile_pool(name="shared", bufs=1))
         psum = ctx.enter_context(tc.psum_pool(name="psum", bufs=1))
 
         def load_list(src, name):
@@ -49,7 +50,7 @@ def tile_picked_zsgn_mean_p_kernel(
             return tile
 
         def load_w1(c, o):
-            tile = keep.tile([P, PACK, CHUNK_WORDS * PACK], F32, name=f"w1_raw{c}_{o}", align_bytes=64)
+            tile = keep.tile([P, PACK, CHUNK_WORDS * PACK], F32, name=f"w1_raw{c}_{o}", tag=f"raw{c}_{o}", align_bytes=64)
             first = c * CHUNK_STEP * PACK
             rows = w1[o * K_PASS : (o + 1) * K_PASS, first : first + CHUNK_WORDS * PACK]
             nc.sync.dma_start(tile[:], rows.rearrange("(p j) c -> p j c", j=PACK))
@@ -71,10 +72,13 @@ def tile_picked_zsgn_mean_p_kernel(
         for o in range(PASSES):
             w1_raw[0, o] = load_w1(0, o)
         x_window.append(load_words(1))
-        friends = [load_list(src, name) for src, name in ((pos1, "pos1"), (pos2, "pos2"), (pos3, "pos3"))]
-        for o in range(PASSES):
-            w1_raw[1, o] = load_w1(1, o)
-        foes = [load_list(src, name) for src, name in ((foe1, "foe1"), (foe2, "foe2"), (foe3, "foe3"))]
+        friends, foes = [load_list(pos1, "pos1")], [load_list(foe1, "foe1")]
+        friends.append(load_list(pos2, "pos2"))
+        w1_raw[1, 0] = load_w1(1, 0)
+        foes.append(load_list(foe2, "foe2"))
+        w1_raw[1, 1] = load_w1(1, 1)
+        friends.append(load_list(pos3, "pos3"))
+        foes.append(load_list(foe3, "foe3"))
         for o in range(PASSES):
             w1_raw[2, o] = load_w1(2, o)
         w_words = []
@@ -96,39 +100,44 @@ def tile_picked_zsgn_mean_p_kernel(
 
         w1_codes, w1_scale = {}, {}
 
-        def quantise_w1(t, o):
-            stage = keep.tile([P, P + 2 * ALIGN, PACK], BF16, name=f"w1_grouped{t}_{o}", tag=f"stage{t}_{o}", align_bytes=64)
-            grouped = stage[:, ALIGN : ALIGN + P, :]
-            if t < TURNED:
-                lead = t * P - TURNED * CHUNK_STEP * t
-                m0, m1 = lead // TURNED, (lead + P - 1) // TURNED + 1
-                first = ALIGN - (lead - TURNED * m0)
-                dst = stage[:, first : first + TURNED * (m1 - m0), :].rearrange("p (m i) j -> p m j i", i=TURNED)
-                src = w1_raw[t, o][:, m0:m1, :, 0:TURNED]
-                if (t, o) == (0, 1):
-                    nc.scalar.copy(dst[:, :SCALAR_WORDS], src[:, :SCALAR_WORDS])
-                    nc.vector.tensor_copy(dst[:, SCALAR_WORDS:], src[:, SCALAR_WORDS:])
-                else:
-                    nc.scalar.copy(dst, src)
+        def cast_turned(t, o, stage, start):
+            lead = t * P - TURNED * CHUNK_STEP * t
+            m0, m1 = lead // TURNED, (lead + P - 1) // TURNED + 1
+            first = start - (lead - TURNED * m0)
+            dst = stage[:, first : first + TURNED * (m1 - m0), :].rearrange("p (m i) j -> p m j i", i=TURNED)
+            src = w1_raw[t, o][:, m0:m1, :, 0:TURNED]
+            if (t, o) == (0, 1):
+                nc.scalar.copy(dst[:, :SCALAR_WORDS], src[:, :SCALAR_WORDS])
+                nc.vector.tensor_copy(dst[:, SCALAR_WORDS:], src[:, SCALAR_WORDS:])
             else:
-                done = 0
-                for c in range(TURNED):
-                    m0 = done - c * CHUNK_STEP
-                    count = CHUNK_WORDS - m0
-                    nc.scalar.copy(grouped[:, done : done + count, :], w1_raw[c, o][:, m0:CHUNK_WORDS, :, TURNED])
-                    done += count
-            w1_codes[t, o] = keep.tile(
-                [P, P], U32, name=f"w1_codes{t}_{o}", tag="stage1_1" if (t, o) == (0, 1) else f"w1_codes{t}_{o}", align_bytes=64
-            )
-            w1_scale[t, o] = keep.tile(
-                [P, P], U8, name=f"w1_scale{t}_{o}", tag="stage1_0" if (t, o) == (0, 1) else f"w1_scale{t}_{o}", align_bytes=64
-            )
-            nc.vector.quantize_mx(
-                out=w1_codes[t, o][:].bitcast(FP8X4), scales=w1_scale[t, o][:], in_=grouped.rearrange("p c j -> p (c j)")
-            )
+                nc.scalar.copy(dst, src)
 
-        for o in range(PASSES):
-            quantise_w1(0, o)
+        def cast_plane(c, o):
+            m0 = 0 if c == 0 else CHUNK_WORDS - CHUNK_STEP
+            done = c * CHUNK_STEP + m0
+            nc.scalar.copy(plane_stage[:, o, done : done + CHUNK_WORDS - m0, :], w1_raw[c, o][:, m0:CHUNK_WORDS, :, TURNED])
+
+        def quantise(codes, scale, grouped):
+            nc.vector.quantize_mx(out=codes[:].bitcast(FP8X4), scales=scale[:], in_=grouped.rearrange("p c j -> p (c j)"))
+
+        def sbuf(shape, dtype, name, offset=None, tag=None):
+            if offset is None:
+                return keep.tile(shape, dtype, name=name, tag=tag or name, align_bytes=64)
+            return shared.tile(shape, dtype, name=name, align_bytes=64, offset=offset)
+
+        def prepare_pass(t, o, stage_at=None, codes_at=None, scale_at=None, codes_tag=None, plane=True):
+            stage = sbuf([P, P + 2 * ALIGN, PACK], BF16, f"stage{t}_{o}", stage_at)
+            cast_turned(t, o, stage, ALIGN)
+            if plane:
+                cast_plane(t, o)
+            codes = sbuf([P, P], U32, f"w1_codes{t}_{o}", codes_at, codes_tag)
+            scale = sbuf([P, P], U8, f"w1_scale{t}_{o}", scale_at)
+            quantise(codes, scale, stage[:, ALIGN : ALIGN + P, :])
+            w1_codes[t, o], w1_scale[t, o] = codes[:], scale[:]
+
+        prepare_pass(0, 0, plane=False)
+        prepare_pass(0, 1, codes_at=1088, scale_at=2688, plane=False)
+        plane_stage = sbuf([P, PASSES, P, PACK], BF16, "plane_stage", 2752)
         pieces = ((0, 256), (256, 128), (384, 128))
         x_all.append(keep.tile([P, S], U32, name="x_codes1", tag="stage0_1", align_bytes=64))
         for first, width in pieces:
@@ -138,54 +147,70 @@ def tile_picked_zsgn_mean_p_kernel(
 
         h = [keep.tile([P, S], F32, name=f"h{t}", align_bytes=64) for t in range(TILES)]
 
-        def hidden(t, first, width, tag):
+        def hidden(t, first, width, tag, on_vector=False):
             acc = psum.tile([P, width], F32, name=tag, tag=tag)
             cols = slice(first, first + width)
             for o in range(PASSES):
                 nc.tensor.matmul_mx(
                     out=acc[:],
-                    lhsT=w1_codes[t, o][:].bitcast(FP8X4),
-                    lhsT_scale=w1_scale[t, o][:],
+                    lhsT=w1_codes[t, o].bitcast(FP8X4),
+                    lhsT_scale=w1_scale[t, o],
                     rhs=x_all[o][:, cols].bitcast(FP8X4),
                     rhs_scale=x_scale[4 * o : P, cols],
                     start=(o == 0),
                     stop=(o == PASSES - 1),
                 )
-            nc.scalar.activation(h[t][:, cols], acc[:], ACT.Relu)
+            if on_vector:
+                nc.vector.tensor_scalar(h[t][:, cols], acc[:], 0.0, None, ALU.max)
+            else:
+                nc.scalar.activation(h[t][:, cols], acc[:], ACT.Relu)
 
         for (first, width), tag in zip(pieces, ("bank0", "bank1", "bank7")):
-            hidden(0, first, width, tag)
-        for t in range(1, TILES):
-            for o in range(PASSES):
-                quantise_w1(t, o)
-            if t == 1:
-                for s in range(2):
-                    hidden(t, s * S // 2, S // 2, f"bank{6 + s}")
-            else:
-                hidden(t, 0, S, f"bank{t - 2}")
+            hidden(0, first, width, tag, on_vector=(first + width == S))
+        prepare_pass(1, 0, stage_at=0)
+        prepare_pass(1, 1, stage_at=1536, codes_tag="stage2_1")
+        for o in range(PASSES):
+            cast_plane(0, o)
+        for s in range(2):
+            hidden(1, s * S // 2, S // 2, f"bank{6 + s}")
+        for o in range(PASSES):
+            prepare_pass(2, o)
+        codes, scale = sbuf([P, PASSES * P], U32, "w1_codes3"), sbuf([P, PASSES * P], U8, "w1_scale3")
+        quantise(codes, scale, plane_stage[:].rearrange("p o c j -> p (o c) j"))
+        for o in range(PASSES):
+            w1_codes[3, o], w1_scale[3, o] = codes[:, o * P : (o + 1) * P], scale[:, o * P : (o + 1) * P]
+        for s in range(2):
+            hidden(2, s * S // 2, S // 2, f"bank{s}")
+        hidden(3, 0, S, "bank6")
 
         mean_t = [[keep.tile([P, 2, P, 2], BF16, name=f"mean_t{z}_{b}", align_bytes=64) for b in range(HALVES)] for z in range(2)]
 
-        def turned_sums(z, t, banks, first, groups):
-            for ds, tag in groups:
-                got_all = keep.tile([P, len(ds), V], F32, name=f"got{z}_{t}_{ds[0]}", tag=tag or f"got{z}_{t}_{ds[0]}", align_bytes=64)
-                for i, d in enumerate(ds):
-                    got = got_all[:, i, :]
-                    nc.vector.tensor_copy(got, h[t][:].indirect(lists[z][d][:]))
-                    for b in range(HALVES):
-                        nc.tensor.matmul(
-                            banks[b][:, first : first + P],
-                            lhsT=got[:, b * P : (b + 1) * P],
-                            rhs=ident[:],
-                            is_transpose=True,
-                            start=(d == 0),
-                            stop=(d == DEGREE - 1),
-                        )
+        def room(count, name, tag=None):
+            tile = keep.tile([P, count, V], F32, name=name, tag=tag or name, align_bytes=64)
+            return [tile[:, i, :] for i in range(count)]
 
-        def round_turned(z, b, bank):
-            src = bank[:].rearrange("v (p j) -> v p j", j=TURNED)
-            nc.scalar.activation(mean_t[z][b][:, 0, :, :], src[:, :, 0:2], ACT.Copy, scale=1.0 / DEGREE)
-            nc.scalar.activation(mean_t[z][b][:, 1, :, :], src[:, :, 2:3].to_broadcast([P, P, 2]), ACT.Copy, scale=1.0 / DEGREE)
+        def fetch(z, t, d, rooms, first=0, width=V):
+            cols = slice(first, first + width)
+            window = h[t][:].indirect(lists[z][d][:, first // 16 : (first + width) // 16])
+            if d == 0:
+                nc.vector.tensor_copy(rooms[d][:, cols], window)
+            else:
+                nc.vector.tensor_tensor(rooms[d][:, cols], window, rooms[d - 1][:, cols], ALU.add)
+
+        def turned_sums(t, rooms):
+            for d in range(DEGREE):
+                for z in range(2):
+                    fetch(z, t, d, rooms[z])
+                    if d == DEGREE - 1:
+                        for b in range(HALVES):
+                            nc.tensor.transpose(sums[z][b][:, t * P : (t + 1) * P], rooms[z][d][:, b * P : (b + 1) * P], ident[:])
+
+        def round_turned(z, b, p0, p1):
+            src = sums[z][b][:].rearrange("v (p j) -> v p j", j=TURNED)[:, p0:p1, :]
+            nc.scalar.activation(mean_t[z][b][:, 0, p0:p1, :], src[:, :, 0:2], ACT.Copy, scale=1.0 / DEGREE)
+            nc.scalar.activation(
+                mean_t[z][b][:, 1, p0:p1, :], src[:, :, 2:3].to_broadcast([P, p1 - p0, 2]), ACT.Copy, scale=1.0 / DEGREE
+            )
 
         z_grouped, z_codes, z_scale = {}, {}, {}
 
@@ -217,40 +242,38 @@ def tile_picked_zsgn_mean_p_kernel(
             [psum.tile([P, TURNED * P], F32, name=f"sum{z}_{b}", tag=f"bank{2 + 2 * z + b}") for b in range(HALVES)]
             for z in range(2)
         ]
-        turned_sums(0, 0, sums[0], 0, (((0, 1), None), ((2,), "stage1_0")))
-        turned_sums(1, 0, sums[1], 0, (((0, 1, 2), "stage1_1"),))
-        turned_sums(0, 1, sums[0], P, (((0,), None), ((1, 2), "stage2_0")))
-        turned_sums(1, 1, sums[1], P, (((0, 1, 2), "stage2_1"),))
-        turned_sums(1, 2, sums[1], 2 * P, (((0,), None), ((1, 2), "stage3_0")))
-        for b in range(HALVES):
-            round_turned(1, b, sums[1][b])
-            turn_back(1, b, f"bank{b}")
-        turned_sums(0, 2, sums[0], 2 * P, (((0, 1, 2), "stage3_1"),))
-        for b in range(HALVES):
-            round_turned(0, b, sums[0][b])
-        last = [psum.tile([P, P], F32, name=f"last{b}", tag=f"bank{6 + b}") for b in range(HALVES)]
-        turned_sums(0, 3, last, 0, (((0, 1, 2), None),))
-        for b in range(HALVES):
-            nc.scalar.activation(mean_t[0][b][:, 1, :, 1], last[b][:], ACT.Copy, scale=1.0 / DEGREE)
-            turn_back(0, b, f"bank{4 + b}")
-
-        part = [keep.tile([P, V], F32, name=f"part{d}", align_bytes=64) for d in range(DEGREE)]
-        for d in range(DEGREE):
+        held = room(2, "got0b", "raw1_1")
+        turned_sums(0, (room(1, "f0") + room(1, "got0a", "raw1_0") + held[:1], room(1, "e0") + held[1:] + room(1, "e02")))
+        held = room(2, "got1a", "raw2_1")
+        turned_sums(1, (room(1, "f1") + held[:1] + room(1, "f12"), room(1, "e1") + held[1:] + room(1, "e12")))
+        early = 2 * P // TURNED
+        for z in range(2):
             for b in range(HALVES):
-                cols = slice(b * P, (b + 1) * P)
-                window = h[TURNED][:].indirect(foes[d][:, b * P // 16 : (b + 1) * P // 16])
-                if d == 0:
-                    nc.vector.tensor_copy(part[d][:, cols], window)
-                else:
-                    nc.vector.tensor_tensor(part[d][:, cols], window, part[d - 1][:, cols], ALU.add)
+                round_turned(z, b, 0, early)
+        turned_sums(2, (room(3, "f2"), room(3, "e2")))
+        for z in range(2):
+            for b in range(HALVES):
+                round_turned(z, b, early, P)
+                turn_back(z, b, f"bank{(0, 1, 6, 7)[2 * z + b]}")
+
+        def plane(z, b):
+            return z_grouped[z, b][:].rearrange("p (v j) -> p v j", j=PACK)[:, :, TURNED]
+
+        part = (room(3, "f3"), room(3, "e3"))
+        for d in range(DEGREE - 1):
+            for z in range(2):
+                fetch(z, TURNED, d, part[z])
+        fetch(0, TURNED, DEGREE - 1, part[0])
         for b in range(HALVES):
-            plane = z_grouped[1, b][:].rearrange("p (v j) -> p v j", j=PACK)[:, :, TURNED]
-            nc.vector.tensor_scalar(plane, part[DEGREE - 1][:, b * P : (b + 1) * P], 1.0 / DEGREE, None, ALU.mult)
+            nc.scalar.activation(plane(0, b), part[0][DEGREE - 1][:, b * P : (b + 1) * P], ACT.Copy, scale=1.0 / DEGREE)
+        for b in range(HALVES):
+            fetch(1, TURNED, DEGREE - 1, part[1], b * P, P)
+        for b in range(HALVES):
+            nc.vector.tensor_scalar(plane(1, b), part[1][DEGREE - 1][:, b * P : (b + 1) * P], 1.0 / DEGREE, None, ALU.mult)
         acc = [psum.tile([P, P], F32, name=f"acc_out{b}", tag=f"bank{2 + b}") for b in range(HALVES)]
         for b in range(HALVES):
             quantise_mean(0, b)
             product(0, b, acc[b])
-        for b in range(HALVES):
             quantise_mean(1, b)
             product(1, b, acc[b])
             result = keep.tile([P, P], F32, name=f"result{b}", align_bytes=64)

@@ -36,7 +36,6 @@ def tile_picked_zsgn_mean_p_kernel(
     nc = tc.nc
     with ExitStack() as ctx:
         keep = ctx.enter_context(tc.tile_pool(name="keep", bufs=1))
-        shared = ctx.enter_context(tc.tile_pool(name="shared", bufs=1))
         psum = ctx.enter_context(tc.psum_pool(name="psum", bufs=1))
 
         def load_list(src, name):
@@ -72,11 +71,11 @@ def tile_picked_zsgn_mean_p_kernel(
         for o in range(PASSES):
             w1_raw[0, o] = load_w1(0, o)
         x_window.append(load_words(1))
-        friends, foes = [load_list(pos1, "pos1")], [load_list(foe1, "foe1")]
-        friends.append(load_list(pos2, "pos2"))
         w1_raw[1, 0] = load_w1(1, 0)
-        foes.append(load_list(foe2, "foe2"))
+        friends, foes = [load_list(pos1, "pos1")], [load_list(foe1, "foe1")]
         w1_raw[1, 1] = load_w1(1, 1)
+        friends.append(load_list(pos2, "pos2"))
+        foes.append(load_list(foe2, "foe2"))
         friends.append(load_list(pos3, "pos3"))
         foes.append(load_list(foe3, "foe3"))
         for o in range(PASSES):
@@ -120,26 +119,23 @@ def tile_picked_zsgn_mean_p_kernel(
         def quantise(codes, scale, grouped):
             nc.vector.quantize_mx(out=codes[:].bitcast(FP8X4), scales=scale[:], in_=grouped.rearrange("p c j -> p (c j)"))
 
-        def sbuf(shape, dtype, name, offset=None, tag=None):
-            if offset is None:
-                return keep.tile(shape, dtype, name=name, tag=tag or name, align_bytes=64)
-            return shared.tile(shape, dtype, name=name, align_bytes=64, offset=offset)
+        def sbuf(shape, dtype, name, tag=None):
+            return keep.tile(shape, dtype, name=name, tag=tag or name, align_bytes=64)
 
-        def prepare_pass(t, o, stage_at=None, codes_at=None, scale_at=None, codes_tag=None, plane=True):
-            stage = sbuf([P, P + 2 * ALIGN, PACK], BF16, f"stage{t}_{o}", stage_at)
+        def prepare_pass(t, o, codes_tag=None, scale_tag=None):
+            stage = sbuf([P, P + 2 * ALIGN, PACK], BF16, f"stage{t}_{o}")
             cast_turned(t, o, stage, ALIGN)
-            if plane:
-                cast_plane(t, o)
-            codes = sbuf([P, P], U32, f"w1_codes{t}_{o}", codes_at, codes_tag)
-            scale = sbuf([P, P], U8, f"w1_scale{t}_{o}", scale_at)
+            cast_plane(t, o)
+            codes = sbuf([P, P], U32, f"w1_codes{t}_{o}", codes_tag)
+            scale = sbuf([P, P], U8, f"w1_scale{t}_{o}", scale_tag)
             quantise(codes, scale, stage[:, ALIGN : ALIGN + P, :])
             w1_codes[t, o], w1_scale[t, o] = codes[:], scale[:]
 
-        prepare_pass(0, 0, plane=False)
-        prepare_pass(0, 1, codes_at=1088, scale_at=2688, plane=False)
-        plane_stage = sbuf([P, PASSES, P, PACK], BF16, "plane_stage", 2752)
+        plane_stage = sbuf([P, PASSES, P, PACK], BF16, "plane_stage")
+        for o in range(PASSES):
+            prepare_pass(0, o)
         pieces = ((0, 256), (256, 128), (384, 128))
-        x_all.append(keep.tile([P, S], U32, name="x_codes1", tag="stage0_1", align_bytes=64))
+        x_all.append(keep.tile([P, S], U32, name="x_codes1", tag="raw0_1", align_bytes=64))
         for first, width in pieces:
             nc.vector.tensor_copy(
                 x_all[1][:, first : first + width], x_window[1][:].indirect(picked[:, first // 16 : (first + width) // 16])
@@ -166,11 +162,9 @@ def tile_picked_zsgn_mean_p_kernel(
                 nc.scalar.activation(h[t][:, cols], acc[:], ACT.Relu)
 
         for (first, width), tag in zip(pieces, ("bank0", "bank1", "bank7")):
-            hidden(0, first, width, tag, on_vector=(first + width == S))
-        prepare_pass(1, 0, stage_at=0)
-        prepare_pass(1, 1, stage_at=1536, codes_tag="stage2_1")
-        for o in range(PASSES):
-            cast_plane(0, o)
+            hidden(0, first, width, tag, on_vector=True)
+        prepare_pass(1, 0, scale_tag="w1_scale0_1")
+        prepare_pass(1, 1, codes_tag="stage2_1")
         for s in range(2):
             hidden(1, s * S // 2, S // 2, f"bank{6 + s}")
         for o in range(PASSES):
@@ -197,13 +191,12 @@ def tile_picked_zsgn_mean_p_kernel(
             else:
                 nc.vector.tensor_tensor(rooms[d][:, cols], window, rooms[d - 1][:, cols], ALU.add)
 
-        def turned_sums(t, rooms):
-            for d in range(DEGREE):
-                for z in range(2):
-                    fetch(z, t, d, rooms[z])
-                    if d == DEGREE - 1:
-                        for b in range(HALVES):
-                            nc.tensor.transpose(sums[z][b][:, t * P : (t + 1) * P], rooms[z][d][:, b * P : (b + 1) * P], ident[:])
+        def turned_sums(t, rooms, steps=range(2 * DEGREE)):
+            for d, z in (divmod(step, 2) for step in steps):
+                fetch(z, t, d, rooms[z])
+                if d == DEGREE - 1:
+                    for b in range(HALVES):
+                        nc.tensor.transpose(sums[z][b][:, t * P : (t + 1) * P], rooms[z][d][:, b * P : (b + 1) * P], ident[:])
 
         def round_turned(z, b, p0, p1):
             src = sums[z][b][:].rearrange("v (p j) -> v p j", j=TURNED)[:, p0:p1, :]
@@ -212,28 +205,33 @@ def tile_picked_zsgn_mean_p_kernel(
                 mean_t[z][b][:, 1, p0:p1, :], src[:, :, 2:3].to_broadcast([P, p1 - p0, 2]), ACT.Copy, scale=1.0 / DEGREE
             )
 
-        z_grouped, z_codes, z_scale = {}, {}, {}
+        z_grouped = [keep.tile([P, V * PACK], BF16, name=f"z_grouped{z}", align_bytes=64) for z in range(2)]
+        z_codes = [keep.tile([P, V], U32, name=f"z_codes{z}", align_bytes=64) for z in range(2)]
+        z_scale = [keep.tile([P, V], U8, name=f"z_scale{z}", align_bytes=64) for z in range(2)]
 
         def turn_back(z, b, tag):
             back = psum.tile([P, 2, P], F32, name=f"back{z}_{b}", tag=tag)
             pairs = mean_t[z][b][:].rearrange("v u p e -> v (u p e)").bitcast(F32)
             for u in range(2):
                 nc.tensor.transpose(back[:, u, :], pairs[:, u * P : (u + 1) * P], ident[:])
-            z_grouped[z, b] = keep.tile([P, P * PACK], BF16, name=f"z_grouped{z}_{b}", align_bytes=64)
-            nc.scalar.copy(z_grouped[z, b][:].bitcast(F32).rearrange("p (v u) -> p v u", u=2), back[:].rearrange("p u v -> p v u"))
+            half = z_grouped[z][:, b * P * PACK : (b + 1) * P * PACK]
+            nc.scalar.copy(half.bitcast(F32).rearrange("p (v u) -> p v u", u=2), back[:].rearrange("p u v -> p v u"))
 
-        def quantise_mean(z, b):
-            z_codes[z, b] = keep.tile([P, P], U32, name=f"z_codes{z}_{b}", align_bytes=64)
-            z_scale[z, b] = keep.tile([P, P], U8, name=f"z_scale{z}_{b}", align_bytes=64)
-            nc.vector.quantize_mx(out=z_codes[z, b][:].bitcast(FP8X4), scales=z_scale[z, b][:], in_=z_grouped[z, b][:])
+        def quantise_mean(z, first, width):
+            cols = slice(first, first + width)
+            nc.vector.quantize_mx(
+                out=z_codes[z][:, cols].bitcast(FP8X4),
+                scales=z_scale[z][:, cols],
+                in_=z_grouped[z][:, first * PACK : (first + width) * PACK],
+            )
 
         def product(z, b, acc):
             nc.tensor.matmul_mx(
                 out=acc[:],
                 lhsT=w_words[z][:].bitcast(FP4X4),
                 lhsT_scale=w_scales[:, z * N : (z + 1) * N],
-                rhs=z_codes[z, b][:].bitcast(FP8X4),
-                rhs_scale=z_scale[z, b][:],
+                rhs=z_codes[z][:, b * P : (b + 1) * P].bitcast(FP8X4),
+                rhs_scale=z_scale[z][:, b * P : (b + 1) * P],
                 start=(z == 0),
                 stop=(z == 1),
             )
@@ -243,38 +241,42 @@ def tile_picked_zsgn_mean_p_kernel(
             for z in range(2)
         ]
         held = room(2, "got0b", "raw1_1")
-        turned_sums(0, (room(1, "f0") + room(1, "got0a", "raw1_0") + held[:1], room(1, "e0") + held[1:] + room(1, "e02")))
+        f0 = room(1, "f0")
+        turned_sums(0, (f0 + held[:1] + room(1, "f02"), room(1, "e0") + held[1:] + room(1, "e02")))
         held = room(2, "got1a", "raw2_1")
         turned_sums(1, (room(1, "f1") + held[:1] + room(1, "f12"), room(1, "e1") + held[1:] + room(1, "e12")))
         early = 2 * P // TURNED
         for z in range(2):
             for b in range(HALVES):
                 round_turned(z, b, 0, early)
-        turned_sums(2, (room(3, "f2"), room(3, "e2")))
+        rooms2, part = (room(3, "f2"), room(3, "e2")), (room(3, "f3"), room(3, "e3"))
+        turned_sums(2, rooms2, range(5))
+        fetch(0, TURNED, 0, part[0])
+        turned_sums(2, rooms2, range(5, 6))
         for z in range(2):
             for b in range(HALVES):
                 round_turned(z, b, early, P)
                 turn_back(z, b, f"bank{(0, 1, 6, 7)[2 * z + b]}")
 
-        def plane(z, b):
-            return z_grouped[z, b][:].rearrange("p (v j) -> p v j", j=PACK)[:, :, TURNED]
+        def plane(z, first, width):
+            return z_grouped[z][:].rearrange("p (v j) -> p v j", j=PACK)[:, first : first + width, TURNED]
 
-        part = (room(3, "f3"), room(3, "e3"))
-        for d in range(DEGREE - 1):
-            for z in range(2):
-                fetch(z, TURNED, d, part[z])
-        fetch(0, TURNED, DEGREE - 1, part[0])
-        for b in range(HALVES):
-            nc.scalar.activation(plane(0, b), part[0][DEGREE - 1][:, b * P : (b + 1) * P], ACT.Copy, scale=1.0 / DEGREE)
-        for b in range(HALVES):
-            fetch(1, TURNED, DEGREE - 1, part[1], b * P, P)
-        for b in range(HALVES):
-            nc.vector.tensor_scalar(plane(1, b), part[1][DEGREE - 1][:, b * P : (b + 1) * P], 1.0 / DEGREE, None, ALU.mult)
+        fetch(0, TURNED, 1, part[0])
+        fetch(1, TURNED, 0, part[1])
+        fetch(0, TURNED, 2, part[0])
+        nc.scalar.activation(plane(0, 0, V), part[0][2], ACT.Copy, scale=1.0 / DEGREE)
+        fetch(1, TURNED, 1, part[1], 0, P)
+        fetch(1, TURNED, 1, part[1], P, P)
+        fetch(1, TURNED, 2, part[1], 0, P)
+        nc.scalar.activation(plane(1, 0, P), part[1][2][:, :P], ACT.Copy, scale=1.0 / DEGREE)
+        fetch(1, TURNED, 2, part[1], P, P)
+        quantise_mean(0, 0, V)
+        nc.vector.tensor_scalar(plane(1, P, P), part[1][2][:, P:], 1.0 / DEGREE, None, ALU.mult)
         acc = [psum.tile([P, P], F32, name=f"acc_out{b}", tag=f"bank{2 + b}") for b in range(HALVES)]
         for b in range(HALVES):
-            quantise_mean(0, b)
             product(0, b, acc[b])
-            quantise_mean(1, b)
+        for b in range(HALVES):
+            quantise_mean(1, b * P, P)
             product(1, b, acc[b])
             result = keep.tile([P, P], F32, name=f"result{b}", align_bytes=64)
             nc.scalar.activation(result[:], acc[b][:], ACT.Tanh)

@@ -62,8 +62,8 @@ def tile_picked_zsgn_mean_p_kernel(
         ident = keep.tile([P, P], F32, name="ident", align_bytes=64)
         make_identity(nc, ident[:])
 
-        picked = load_list(offs, "offs")
         x_window = [load_words(0)]
+        picked = load_list(offs, "offs")
         for q in range(4):
             rows = slice(32 * q, 32 * q + 4 * PASSES)
             nc.sync.dma_start(scale_window[rows, :].bitcast(I32), x_scales[:, 4 * q : 4 * q + 4, :].bitcast(I32))
@@ -78,18 +78,7 @@ def tile_picked_zsgn_mean_p_kernel(
         foes.append(load_list(foe2, "foe2"))
         friends.append(load_list(pos3, "pos3"))
         foes.append(load_list(foe3, "foe3"))
-        for o in range(PASSES):
-            w1_raw[2, o] = load_w1(2, o)
-        w_words = []
-        for z, (words, scales) in enumerate(((w2_words, w2_scales), (w3_words, w3_scales))):
-            tile = keep.tile([P, 2 * N], U8, name=f"w_words{z}", align_bytes=64)
-            nc.sync.dma_start(tile[:].bitcast(I32), words[0].bitcast(I32))
-            w_words.append(tile)
-            for q in range(4):
-                nc.sync.dma_start(
-                    w_scales[32 * q : 32 * q + 4, z * N : (z + 1) * N].bitcast(I32),
-                    scales[0, 4 * q : 4 * q + 4, :].bitcast(I32),
-                )
+        w1_raw[2, 0] = load_w1(2, 0)
         lists = [friends, foes]
 
         x_all = [keep.tile([P, S], U32, name="x_codes0", align_bytes=64)]
@@ -122,11 +111,11 @@ def tile_picked_zsgn_mean_p_kernel(
         def sbuf(shape, dtype, name, tag=None):
             return keep.tile(shape, dtype, name=name, tag=tag or name, align_bytes=64)
 
-        def prepare_pass(t, o, codes_tag=None, scale_tag=None):
-            stage = sbuf([P, P + 2 * ALIGN, PACK], BF16, f"stage{t}_{o}")
+        def prepare_pass(t, o, stage_tag=None, scale_tag=None):
+            stage = sbuf([P, P + 2 * ALIGN, PACK], BF16, f"stage{t}_{o}", stage_tag)
             cast_turned(t, o, stage, ALIGN)
             cast_plane(t, o)
-            codes = sbuf([P, P], U32, f"w1_codes{t}_{o}", codes_tag)
+            codes = sbuf([P, P], U32, f"w1_codes{t}_{o}")
             scale = sbuf([P, P], U8, f"w1_scale{t}_{o}", scale_tag)
             quantise(codes, scale, stage[:, ALIGN : ALIGN + P, :])
             w1_codes[t, o], w1_scale[t, o] = codes[:], scale[:]
@@ -164,7 +153,18 @@ def tile_picked_zsgn_mean_p_kernel(
         for (first, width), tag in zip(pieces, ("bank0", "bank1", "bank7")):
             hidden(0, first, width, tag, on_vector=True)
         prepare_pass(1, 0, scale_tag="w1_scale0_1")
-        prepare_pass(1, 1, codes_tag="stage2_1")
+        prepare_pass(1, 1, stage_tag="raw2_1")
+        w1_raw[2, 1] = load_w1(2, 1)
+        w_words = []
+        for z, (words, scales) in enumerate(((w2_words, w2_scales), (w3_words, w3_scales))):
+            tile = keep.tile([P, 2 * N], U8, name=f"w_words{z}", align_bytes=64)
+            nc.sync.dma_start(tile[:].bitcast(I32), words[0].bitcast(I32))
+            w_words.append(tile)
+            for q in range(4):
+                nc.sync.dma_start(
+                    w_scales[32 * q : 32 * q + 4, z * N : (z + 1) * N].bitcast(I32),
+                    scales[0, 4 * q : 4 * q + 4, :].bitcast(I32),
+                )
         for s in range(2):
             hidden(1, s * S // 2, S // 2, f"bank{6 + s}")
         for o in range(PASSES):
@@ -241,8 +241,7 @@ def tile_picked_zsgn_mean_p_kernel(
             for z in range(2)
         ]
         held = room(2, "got0b", "raw1_1")
-        f0 = room(1, "f0")
-        turned_sums(0, (f0 + held[:1] + room(1, "f02"), room(1, "e0") + held[1:] + room(1, "e02")))
+        turned_sums(0, (room(1, "f0") + held[:1] + room(1, "f02"), room(1, "e0") + held[1:] + room(1, "e02")))
         held = room(2, "got1a", "raw2_1")
         turned_sums(1, (room(1, "f1") + held[:1] + room(1, "f12"), room(1, "e1") + held[1:] + room(1, "e12")))
         early = 2 * P // TURNED

@@ -26,8 +26,11 @@ HALVES = V // P
 DEGREE = 3
 CHUNK_STEP, CHUNK_WORDS = 42, 44
 TURNED = PACK - 1
-ALIGN = 8
-SCALAR_WORDS = 21
+PAIR_FIRST = (0, 43, 86, P)
+SINGLE_FIRST = (0, 42, 84, P)
+STAGE_COLS = 704
+RAW_BYTES = PACK * CHUNK_WORDS * PACK * 4
+OVERLAP = 64
 
 
 def tile_picked_zsgn_mean_p_kernel(
@@ -36,6 +39,7 @@ def tile_picked_zsgn_mean_p_kernel(
     nc = tc.nc
     with ExitStack() as ctx:
         keep = ctx.enter_context(tc.tile_pool(name="keep", bufs=1))
+        placed = ctx.enter_context(tc.tile_pool(name="placed", bufs=1))
         psum = ctx.enter_context(tc.psum_pool(name="psum", bufs=1))
 
         def load_list(src, name):
@@ -48,8 +52,12 @@ def tile_picked_zsgn_mean_p_kernel(
             nc.sync.dma_start(tile[:].bitcast(I32), x_words[o].rearrange("p n t -> p (n t)").bitcast(I32))
             return tile
 
-        def load_w1(c, o):
-            tile = keep.tile([P, PACK, CHUNK_WORDS * PACK], F32, name=f"w1_raw{c}_{o}", tag=f"raw{c}_{o}", align_bytes=64)
+        def load_w1(c, o, offset=None):
+            shape = [P, PACK, CHUNK_WORDS * PACK]
+            if offset is None:
+                tile = keep.tile(shape, F32, name=f"w1_raw{c}_{o}", tag=f"raw{c}_{o}", align_bytes=64)
+            else:
+                tile = placed.tile(shape, F32, name=f"w1_raw{c}_{o}", offset=offset, align_bytes=64)
             first = c * CHUNK_STEP * PACK
             rows = w1[o * K_PASS : (o + 1) * K_PASS, first : first + CHUNK_WORDS * PACK]
             nc.sync.dma_start(tile[:], rows.rearrange("(p j) c -> p j c", j=PACK))
@@ -73,7 +81,7 @@ def tile_picked_zsgn_mean_p_kernel(
         x_window.append(load_words(1))
         w1_raw[1, 0] = load_w1(1, 0)
         friends, foes = [load_list(pos1, "pos1")], [load_list(foe1, "foe1")]
-        w1_raw[1, 1] = load_w1(1, 1)
+        w1_raw[1, 1] = load_w1(1, 1, RAW_BYTES)
         friends.append(load_list(pos2, "pos2"))
         foes.append(load_list(foe2, "foe2"))
         friends.append(load_list(pos3, "pos3"))
@@ -88,22 +96,24 @@ def tile_picked_zsgn_mean_p_kernel(
 
         w1_codes, w1_scale = {}, {}
 
-        def cast_turned(t, o, stage, start):
-            lead = t * P - TURNED * CHUNK_STEP * t
-            m0, m1 = lead // TURNED, (lead + P - 1) // TURNED + 1
-            first = start - (lead - TURNED * m0)
-            dst = stage[:, first : first + TURNED * (m1 - m0), :].rearrange("p (m i) j -> p m j i", i=TURNED)
-            src = w1_raw[t, o][:, m0:m1, :, 0:TURNED]
-            if (t, o) == (0, 1):
-                nc.scalar.copy(dst[:, :SCALAR_WORDS], src[:, :SCALAR_WORDS])
-                nc.vector.tensor_copy(dst[:, SCALAR_WORDS:], src[:, SCALAR_WORDS:])
+        def cast_pairs(t, o):
+            g0, g1 = PAIR_FIRST[t], PAIR_FIRST[t + 1]
+            dst = stage[o][:, t * P : t * P + 2 * (g1 - g0), :].rearrange("p (m i) j -> p m j i", i=2)
+            nc.scalar.copy(dst, w1_raw[t, o][:, g0 - t * CHUNK_STEP : g1 - t * CHUNK_STEP, :, 0:2])
+
+        def cast_singles(t, o):
+            g0, g1 = SINGLE_FIRST[t], SINGLE_FIRST[t + 1]
+            first = (t + 1) * P - (g1 - g0)
+            apart = TURNED * P + g0 - first
+            dst = stage[o][:, first : first + 2 * apart, :].rearrange("p (i m) j -> p m j i", i=2)[:, : g1 - g0]
+            src = w1_raw[t, o][:, : g1 - g0, :, 2:PACK]
+            if t > 0 and o == PASSES - 1:
+                for i in range(2):
+                    nc.scalar.copy(dst[:, :, :, i], src[:, :, :, i])
+            elif o == PASSES - 1:
+                nc.vector.tensor_copy(dst, src)
             else:
                 nc.scalar.copy(dst, src)
-
-        def cast_plane(c, o):
-            m0 = 0 if c == 0 else CHUNK_WORDS - CHUNK_STEP
-            done = c * CHUNK_STEP + m0
-            nc.scalar.copy(plane_stage[:, o, done : done + CHUNK_WORDS - m0, :], w1_raw[c, o][:, m0:CHUNK_WORDS, :, TURNED])
 
         def quantise(codes, scale, grouped):
             nc.vector.quantize_mx(out=codes[:].bitcast(FP8X4), scales=scale[:], in_=grouped.rearrange("p c j -> p (c j)"))
@@ -111,23 +121,33 @@ def tile_picked_zsgn_mean_p_kernel(
         def sbuf(shape, dtype, name, tag=None):
             return keep.tile(shape, dtype, name=name, tag=tag or name, align_bytes=64)
 
-        def prepare_pass(t, o, stage_tag=None, scale_tag=None):
-            stage = sbuf([P, P + 2 * ALIGN, PACK], BF16, f"stage{t}_{o}", stage_tag)
-            cast_turned(t, o, stage, ALIGN)
-            cast_plane(t, o)
-            codes = sbuf([P, P], U32, f"w1_codes{t}_{o}")
-            scale = sbuf([P, P], U8, f"w1_scale{t}_{o}", scale_tag)
-            quantise(codes, scale, stage[:, ALIGN : ALIGN + P, :])
-            w1_codes[t, o], w1_scale[t, o] = codes[:], scale[:]
+        def prepare_pass(t, o, scale_tag=None, tiles=1):
+            cast_pairs(t, o)
+            cast_singles(t, o)
+            quantise_pass(t, o, scale_tag, tiles)
 
-        plane_stage = sbuf([P, PASSES, P, PACK], BF16, "plane_stage")
+        def quantise_pass(t, o, scale_tag=None, tiles=1):
+            codes = sbuf([P, tiles * P], U32, f"w1_codes{t}_{o}")
+            scale = sbuf([P, tiles * P], U8, f"w1_scale{t}_{o}", scale_tag)
+            quantise(codes, scale, stage[o][:, t * P : (t + tiles) * P, :])
+            for n in range(tiles):
+                w1_codes[t + n, o], w1_scale[t + n, o] = codes[:, n * P : (n + 1) * P], scale[:, n * P : (n + 1) * P]
+
+        stage = [sbuf([P, STAGE_COLS, PACK], BF16, f"stage{o}") for o in range(PASSES)]
         for o in range(PASSES):
             prepare_pass(0, o)
         pieces = ((0, 256), (256, 128), (384, 128))
-        x_all.append(keep.tile([P, S], U32, name="x_codes1", tag="raw0_1", align_bytes=64))
+        x_late = [keep.tile([P, S // 2], U32, name=f"x_codes1_{s}", tag=f"raw0_{s}", align_bytes=64) for s in range(2)]
+
+        def picked_words(o, first, width):
+            if o == 0:
+                return x_all[0][:, first : first + width]
+            s, start = divmod(first, S // 2)
+            return x_late[s][:, start : start + width]
+
         for first, width in pieces:
             nc.vector.tensor_copy(
-                x_all[1][:, first : first + width], x_window[1][:].indirect(picked[:, first // 16 : (first + width) // 16])
+                picked_words(1, first, width), x_window[1][:].indirect(picked[:, first // 16 : (first + width) // 16])
             )
 
         h = [keep.tile([P, S], F32, name=f"h{t}", align_bytes=64) for t in range(TILES)]
@@ -135,16 +155,18 @@ def tile_picked_zsgn_mean_p_kernel(
         def hidden(t, first, width, tag, on_vector=False):
             acc = psum.tile([P, width], F32, name=tag, tag=tag)
             cols = slice(first, first + width)
-            for o in range(PASSES):
-                nc.tensor.matmul_mx(
-                    out=acc[:],
-                    lhsT=w1_codes[t, o].bitcast(FP8X4),
-                    lhsT_scale=w1_scale[t, o],
-                    rhs=x_all[o][:, cols].bitcast(FP8X4),
-                    rhs_scale=x_scale[4 * o : P, cols],
-                    start=(o == 0),
-                    stop=(o == PASSES - 1),
-                )
+            group = min(width, S // 2)
+            for start in range(0, width, group):
+                for o in range(PASSES):
+                    nc.tensor.matmul_mx(
+                        out=acc[:, start : start + group],
+                        lhsT=w1_codes[t, o].bitcast(FP8X4),
+                        lhsT_scale=w1_scale[t, o],
+                        rhs=picked_words(o, first + start, group).bitcast(FP8X4),
+                        rhs_scale=x_scale[4 * o : P, first + start : first + start + group],
+                        start=(o == 0),
+                        stop=(o == PASSES - 1),
+                    )
             if on_vector:
                 nc.vector.tensor_scalar(h[t][:, cols], acc[:], 0.0, None, ALU.max)
             else:
@@ -153,8 +175,8 @@ def tile_picked_zsgn_mean_p_kernel(
         for (first, width), tag in zip(pieces, ("bank0", "bank1", "bank7")):
             hidden(0, first, width, tag, on_vector=True)
         prepare_pass(1, 0, scale_tag="w1_scale0_1")
-        prepare_pass(1, 1, stage_tag="raw2_1")
-        w1_raw[2, 1] = load_w1(2, 1)
+        prepare_pass(1, 1)
+        w1_raw[2, 1] = load_w1(2, 1, OVERLAP)
         w_words = []
         for z, (words, scales) in enumerate(((w2_words, w2_scales), (w3_words, w3_scales))):
             tile = keep.tile([P, 2 * N], U8, name=f"w_words{z}", align_bytes=64)
@@ -167,20 +189,20 @@ def tile_picked_zsgn_mean_p_kernel(
                 )
         for s in range(2):
             hidden(1, s * S // 2, S // 2, f"bank{6 + s}")
-        for o in range(PASSES):
-            prepare_pass(2, o)
-        codes, scale = sbuf([P, PASSES * P], U32, "w1_codes3"), sbuf([P, PASSES * P], U8, "w1_scale3")
-        quantise(codes, scale, plane_stage[:].rearrange("p o c j -> p (o c) j"))
-        for o in range(PASSES):
-            w1_codes[3, o], w1_scale[3, o] = codes[:, o * P : (o + 1) * P], scale[:, o * P : (o + 1) * P]
+        prepare_pass(2, 0, tiles=2)
+        prepare_pass(2, 1)
+        quantise_pass(3, 1)
         for s in range(2):
             hidden(2, s * S // 2, S // 2, f"bank{s}")
         hidden(3, 0, S, "bank6")
 
-        mean_t = [[keep.tile([P, 2, P, 2], BF16, name=f"mean_t{z}_{b}", align_bytes=64) for b in range(HALVES)] for z in range(2)]
+        mean_t = [keep.tile([P, HALVES, 2, P, 2], BF16, name=f"mean_t{z}", align_bytes=64) for z in range(2)]
 
-        def room(count, name, tag=None):
-            tile = keep.tile([P, count, V], F32, name=name, tag=tag or name, align_bytes=64)
+        def room(count, name, offset=None):
+            if offset is None:
+                tile = keep.tile([P, count, V], F32, name=name, align_bytes=64)
+            else:
+                tile = placed.tile([P, count, V], F32, name=name, offset=offset, align_bytes=64)
             return [tile[:, i, :] for i in range(count)]
 
         def fetch(z, t, d, rooms, first=0, width=V):
@@ -195,25 +217,41 @@ def tile_picked_zsgn_mean_p_kernel(
             for d, z in (divmod(step, 2) for step in steps):
                 fetch(z, t, d, rooms[z])
                 if d == DEGREE - 1:
-                    for b in range(HALVES):
-                        nc.tensor.transpose(sums[z][b][:, t * P : (t + 1) * P], rooms[z][d][:, b * P : (b + 1) * P], ident[:])
+                    turn(z, t, rooms[z][d])
 
-        def round_turned(z, b, p0, p1):
-            src = sums[z][b][:].rearrange("v (p j) -> v p j", j=TURNED)[:, p0:p1, :]
-            nc.scalar.activation(mean_t[z][b][:, 0, p0:p1, :], src[:, :, 0:2], ACT.Copy, scale=1.0 / DEGREE)
-            nc.scalar.activation(
-                mean_t[z][b][:, 1, p0:p1, :], src[:, :, 2:3].to_broadcast([P, p1 - p0, 2]), ACT.Copy, scale=1.0 / DEGREE
-            )
+        def round_turned(z, t, halves, bank):
+            g0, g1 = PAIR_FIRST[t], PAIR_FIRST[t + 1]
+            pairs = mean_t[z][:, halves, 0, g0:g1, :].rearrange("v b p e -> v b (p e)")
+            nc.scalar.activation(pairs, bank[:, :, : 2 * (g1 - g0)], ACT.Copy, scale=1.0 / DEGREE)
+            g0, g1 = SINGLE_FIRST[t], SINGLE_FIRST[t + 1]
+            singles = bank[:, :, P - (g1 - g0) :].unsqueeze(3).to_broadcast([P, bank.shape[1], g1 - g0, 2])
+            nc.scalar.activation(mean_t[z][:, halves, 1, g0:g1, :], singles, ACT.Copy, scale=1.0 / DEGREE)
 
+        def turn(z, t, total):
+            if t < TURNED - 1:
+                for b in range(HALVES):
+                    nc.tensor.transpose(sums[z][:, t, b, :], total[:, b * P : (b + 1) * P], ident[:])
+                if t == 1:
+                    for n in range(2):
+                        round_turned(z, n, slice(0, HALVES), sums[z][:, n])
+                return
+            banks = [psum.tile([P, 1, P], F32, name=f"late{z}_{b}", tag=f"bank{3 + 2 * z - b}") for b in range(HALVES)]
+            for b in range(HALVES):
+                nc.tensor.transpose(banks[b][:, 0, :], total[:, b * P : (b + 1) * P], ident[:])
+            for b in range(HALVES):
+                round_turned(z, t, slice(b, b + 1), banks[b][:])
+                turn_back(z, b)
+
+        sums = [psum.tile([P, 2, HALVES, P], F32, name=f"sum{z}", tag=f"bank{2 + 2 * z}") for z in range(2)]
         z_grouped = [keep.tile([P, V * PACK], BF16, name=f"z_grouped{z}", align_bytes=64) for z in range(2)]
         z_codes = [keep.tile([P, V], U32, name=f"z_codes{z}", align_bytes=64) for z in range(2)]
         z_scale = [keep.tile([P, V], U8, name=f"z_scale{z}", align_bytes=64) for z in range(2)]
 
-        def turn_back(z, b, tag):
-            back = psum.tile([P, 2, P], F32, name=f"back{z}_{b}", tag=tag)
-            pairs = mean_t[z][b][:].rearrange("v u p e -> v (u p e)").bitcast(F32)
+        def turn_back(z, b):
+            words = mean_t[z][:, b].rearrange("v u p e -> v (u p e)").bitcast(F32)
+            back = psum.tile([P, 2, P], F32, name=f"back{z}_{b}", tag=f"bank{(0, 1, 6, 7)[2 * z + b]}")
             for u in range(2):
-                nc.tensor.transpose(back[:, u, :], pairs[:, u * P : (u + 1) * P], ident[:])
+                nc.tensor.transpose(back[:, u, :], words[:, u * P : (u + 1) * P], ident[:])
             half = z_grouped[z][:, b * P * PACK : (b + 1) * P * PACK]
             nc.scalar.copy(half.bitcast(F32).rearrange("p (v u) -> p v u", u=2), back[:].rearrange("p u v -> p v u"))
 
@@ -236,26 +274,16 @@ def tile_picked_zsgn_mean_p_kernel(
                 stop=(z == 1),
             )
 
-        sums = [
-            [psum.tile([P, TURNED * P], F32, name=f"sum{z}_{b}", tag=f"bank{2 + 2 * z + b}") for b in range(HALVES)]
-            for z in range(2)
-        ]
-        held = room(2, "got0b", "raw1_1")
-        turned_sums(0, (room(1, "f0") + held[:1] + room(1, "f02"), room(1, "e0") + held[1:] + room(1, "e02")))
-        held = room(2, "got1a", "raw2_1")
-        turned_sums(1, (room(1, "f1") + held[:1] + room(1, "f12"), room(1, "e1") + held[1:] + room(1, "e12")))
-        early = 2 * P // TURNED
-        for z in range(2):
-            for b in range(HALVES):
-                round_turned(z, b, 0, early)
+        held = room(2, "got0b", 2 * RAW_BYTES - OVERLAP)
+        rooms0 = (room(1, "f0") + held[:1] + room(1, "f02"), room(1, "e0") + held[1:] + room(1, "e02"))
+        turned_sums(0, rooms0)
+        held = room(2, "got1a", 0)
+        rooms1 = (room(1, "f1") + held[:1] + room(1, "f12"), room(1, "e1") + held[1:] + room(1, "e12"))
         rooms2, part = (room(3, "f2"), room(3, "e2")), (room(3, "f3"), room(3, "e3"))
+        turned_sums(1, rooms1)
         turned_sums(2, rooms2, range(5))
         fetch(0, TURNED, 0, part[0])
-        turned_sums(2, rooms2, range(5, 6))
-        for z in range(2):
-            for b in range(HALVES):
-                round_turned(z, b, early, P)
-                turn_back(z, b, f"bank{(0, 1, 6, 7)[2 * z + b]}")
+        turned_sums(2, rooms2, (5,))
 
         def plane(z, first, width):
             return z_grouped[z][:].rearrange("p (v j) -> p v j", j=PACK)[:, first : first + width, TURNED]

@@ -24,12 +24,15 @@ PASSES = K // K_PASS
 TILES = H // P
 HALVES = V // P
 DEGREE = 3
-CHUNK_STEP, CHUNK_WORDS = 42, 44
-TURNED = PACK - 1
+LIST_ROWS = 16
+QUADRANT = 32
+DIRECT = TILES - 1
+FRIENDS, FOES = 0, 1
 PAIR_FIRST = (0, 43, 86, P)
 SINGLE_FIRST = (0, 42, 84, P)
+CHUNK_STEP, CHUNK_GROUPS = 42, 44
+RAW_BYTES = PACK * CHUNK_GROUPS * PACK * 4
 STAGE_COLS = 704
-RAW_BYTES = PACK * CHUNK_WORDS * PACK * 4
 OVERLAP = 64
 
 
@@ -47,20 +50,24 @@ def tile_picked_zsgn_mean_p_kernel(
             nc.sync.dma_start(tile[:], src)
             return tile
 
+        def entries(list_tile, first, width):
+            return list_tile[:, first // LIST_ROWS : (first + width) // LIST_ROWS]
+
         def load_words(o):
             tile = keep.tile([P, T], U32, name=f"x_window{o}", align_bytes=64)
             nc.sync.dma_start(tile[:].bitcast(I32), x_words[o].rearrange("p n t -> p (n t)").bitcast(I32))
             return tile
 
         def load_w1(c, o, offset=None):
-            shape = [P, PACK, CHUNK_WORDS * PACK]
+            shape = [P, PACK, CHUNK_GROUPS * PACK]
             if offset is None:
                 tile = keep.tile(shape, F32, name=f"w1_raw{c}_{o}", tag=f"raw{c}_{o}", align_bytes=64)
             else:
                 tile = placed.tile(shape, F32, name=f"w1_raw{c}_{o}", offset=offset, align_bytes=64)
             first = c * CHUNK_STEP * PACK
-            rows = w1[o * K_PASS : (o + 1) * K_PASS, first : first + CHUNK_WORDS * PACK]
-            nc.sync.dma_start(tile[:], rows.rearrange("(p j) c -> p j c", j=PACK))
+            width = max(PAIR_FIRST[c + 1], SINGLE_FIRST[c + 1]) * PACK - first
+            rows = w1[o * K_PASS : (o + 1) * K_PASS, first : first + width]
+            nc.sync.dma_start(tile[:, :, :width], rows.rearrange("(p j) c -> p j c", j=PACK))
             return tile[:].rearrange("p j (m i) -> p m j i", i=PACK)
 
         scale_window = keep.tile([P, T], U8, name="scale_window", align_bytes=64)
@@ -72,8 +79,8 @@ def tile_picked_zsgn_mean_p_kernel(
 
         x_window = [load_words(0)]
         picked = load_list(offs, "offs")
-        for q in range(4):
-            rows = slice(32 * q, 32 * q + 4 * PASSES)
+        for q in range(P // QUADRANT):
+            rows = slice(QUADRANT * q, QUADRANT * q + 4 * PASSES)
             nc.sync.dma_start(scale_window[rows, :].bitcast(I32), x_scales[:, 4 * q : 4 * q + 4, :].bitcast(I32))
         w1_raw = {}
         for o in range(PASSES):
@@ -87,10 +94,11 @@ def tile_picked_zsgn_mean_p_kernel(
         friends.append(load_list(pos3, "pos3"))
         foes.append(load_list(foe3, "foe3"))
         w1_raw[2, 0] = load_w1(2, 0)
+        w1_raw[2, 1] = load_w1(2, 1, 0)
         lists = [friends, foes]
 
-        x_all = [keep.tile([P, S], U32, name="x_codes0", align_bytes=64)]
-        nc.vector.tensor_copy(x_all[0][:], x_window[0][:].indirect(picked[:]))
+        x_first = keep.tile([P, S], U32, name="x_codes0", align_bytes=64)
+        nc.vector.tensor_copy(x_first[:], x_window[0][:].indirect(picked[:]))
         x_scale = keep.tile([P, S], U8, name="x_scale", align_bytes=64)
         nc.vector.tensor_copy(x_scale[:], scale_window[:].indirect(picked[:]))
 
@@ -104,7 +112,7 @@ def tile_picked_zsgn_mean_p_kernel(
         def cast_singles(t, o):
             g0, g1 = SINGLE_FIRST[t], SINGLE_FIRST[t + 1]
             first = (t + 1) * P - (g1 - g0)
-            apart = TURNED * P + g0 - first
+            apart = DIRECT * P + g0 - first
             dst = stage[o][:, first : first + 2 * apart, :].rearrange("p (i m) j -> p m j i", i=2)[:, : g1 - g0]
             src = w1_raw[t, o][:, : g1 - g0, :, 2:PACK]
             if t > 0 and o == PASSES - 1:
@@ -115,40 +123,35 @@ def tile_picked_zsgn_mean_p_kernel(
             else:
                 nc.scalar.copy(dst, src)
 
-        def quantise(codes, scale, grouped):
-            nc.vector.quantize_mx(out=codes[:].bitcast(FP8X4), scales=scale[:], in_=grouped.rearrange("p c j -> p (c j)"))
-
-        def sbuf(shape, dtype, name, tag=None):
-            return keep.tile(shape, dtype, name=name, tag=tag or name, align_bytes=64)
-
-        def prepare_pass(t, o, scale_tag=None, tiles=1):
-            cast_pairs(t, o)
-            cast_singles(t, o)
-            quantise_pass(t, o, scale_tag, tiles)
-
         def quantise_pass(t, o, scale_tag=None, tiles=1):
-            codes = sbuf([P, tiles * P], U32, f"w1_codes{t}_{o}")
-            scale = sbuf([P, tiles * P], U8, f"w1_scale{t}_{o}", scale_tag)
-            quantise(codes, scale, stage[o][:, t * P : (t + tiles) * P, :])
+            codes = keep.tile([P, tiles * P], U32, name=f"w1_codes{t}_{o}", align_bytes=64)
+            name = f"w1_scale{t}_{o}"
+            scale = keep.tile([P, tiles * P], U8, name=name, tag=scale_tag or name, align_bytes=64)
+            grouped = stage[o][:, t * P : (t + tiles) * P, :].rearrange("p c j -> p (c j)")
+            nc.vector.quantize_mx(out=codes[:].bitcast(FP8X4), scales=scale[:], in_=grouped)
             for n in range(tiles):
                 w1_codes[t + n, o], w1_scale[t + n, o] = codes[:, n * P : (n + 1) * P], scale[:, n * P : (n + 1) * P]
 
-        stage = [sbuf([P, STAGE_COLS, PACK], BF16, f"stage{o}") for o in range(PASSES)]
+        def prepare_pass(t, o, scale_tag=None):
+            cast_pairs(t, o)
+            cast_singles(t, o)
+            quantise_pass(t, o, scale_tag)
+
+        stage = [keep.tile([P, STAGE_COLS, PACK], BF16, name=f"stage{o}", align_bytes=64) for o in range(PASSES)]
         for o in range(PASSES):
             prepare_pass(0, o)
+
         pieces = ((0, 256), (256, 128), (384, 128))
         x_late = [keep.tile([P, S // 2], U32, name=f"x_codes1_{s}", tag=f"raw0_{s}", align_bytes=64) for s in range(2)]
 
         def picked_words(o, first, width):
             if o == 0:
-                return x_all[0][:, first : first + width]
+                return x_first[:, first : first + width]
             s, start = divmod(first, S // 2)
             return x_late[s][:, start : start + width]
 
         for first, width in pieces:
-            nc.vector.tensor_copy(
-                picked_words(1, first, width), x_window[1][:].indirect(picked[:, first // 16 : (first + width) // 16])
-            )
+            nc.vector.tensor_copy(picked_words(1, first, width), x_window[1][:].indirect(entries(picked, first, width)))
 
         h = [keep.tile([P, S], F32, name=f"h{t}", align_bytes=64) for t in range(TILES)]
 
@@ -176,25 +179,26 @@ def tile_picked_zsgn_mean_p_kernel(
             hidden(0, first, width, tag, on_vector=True)
         prepare_pass(1, 0, scale_tag="w1_scale0_1")
         prepare_pass(1, 1)
-        w1_raw[2, 1] = load_w1(2, 1, OVERLAP)
+        cast_pairs(2, 0)
+        cast_singles(2, 0)
         w_words = []
         for z, (words, scales) in enumerate(((w2_words, w2_scales), (w3_words, w3_scales))):
             tile = keep.tile([P, 2 * N], U8, name=f"w_words{z}", align_bytes=64)
             nc.sync.dma_start(tile[:].bitcast(I32), words[0].bitcast(I32))
             w_words.append(tile)
-            for q in range(4):
+            for q in range(P // QUADRANT):
                 nc.sync.dma_start(
-                    w_scales[32 * q : 32 * q + 4, z * N : (z + 1) * N].bitcast(I32),
+                    w_scales[QUADRANT * q : QUADRANT * q + 4, z * N : (z + 1) * N].bitcast(I32),
                     scales[0, 4 * q : 4 * q + 4, :].bitcast(I32),
                 )
         for s in range(2):
             hidden(1, s * S // 2, S // 2, f"bank{6 + s}")
-        prepare_pass(2, 0, tiles=2)
+        quantise_pass(2, 0, tiles=2)
         prepare_pass(2, 1)
-        quantise_pass(3, 1)
+        quantise_pass(DIRECT, 1)
         for s in range(2):
             hidden(2, s * S // 2, S // 2, f"bank{s}")
-        hidden(3, 0, S, "bank6")
+        hidden(DIRECT, 0, S, "bank6")
 
         mean_t = [keep.tile([P, HALVES, 2, P, 2], BF16, name=f"mean_t{z}", align_bytes=64) for z in range(2)]
 
@@ -207,7 +211,7 @@ def tile_picked_zsgn_mean_p_kernel(
 
         def fetch(z, t, d, rooms, first=0, width=V):
             cols = slice(first, first + width)
-            window = h[t][:].indirect(lists[z][d][:, first // 16 : (first + width) // 16])
+            window = h[t][:].indirect(entries(lists[z][d], first, width))
             if d == 0:
                 nc.vector.tensor_copy(rooms[d][:, cols], window)
             else:
@@ -228,7 +232,7 @@ def tile_picked_zsgn_mean_p_kernel(
             nc.scalar.activation(mean_t[z][:, halves, 1, g0:g1, :], singles, ACT.Copy, scale=1.0 / DEGREE)
 
         def turn(z, t, total):
-            if t < TURNED - 1:
+            if t < DIRECT - 1:
                 for b in range(HALVES):
                     nc.tensor.transpose(sums[z][:, t, b, :], total[:, b * P : (b + 1) * P], ident[:])
                 if t == 1:
@@ -246,10 +250,11 @@ def tile_picked_zsgn_mean_p_kernel(
         z_grouped = [keep.tile([P, V * PACK], BF16, name=f"z_grouped{z}", align_bytes=64) for z in range(2)]
         z_codes = [keep.tile([P, V], U32, name=f"z_codes{z}", align_bytes=64) for z in range(2)]
         z_scale = [keep.tile([P, V], U8, name=f"z_scale{z}", align_bytes=64) for z in range(2)]
+        back_banks = (("bank0", "bank1"), ("bank6", "bank7"))
 
         def turn_back(z, b):
             words = mean_t[z][:, b].rearrange("v u p e -> v (u p e)").bitcast(F32)
-            back = psum.tile([P, 2, P], F32, name=f"back{z}_{b}", tag=f"bank{(0, 1, 6, 7)[2 * z + b]}")
+            back = psum.tile([P, 2, P], F32, name=f"back{z}_{b}", tag=back_banks[z][b])
             for u in range(2):
                 nc.tensor.transpose(back[:, u, :], words[:, u * P : (u + 1) * P], ident[:])
             half = z_grouped[z][:, b * P * PACK : (b + 1) * P * PACK]
@@ -270,8 +275,8 @@ def tile_picked_zsgn_mean_p_kernel(
                 lhsT_scale=w_scales[:, z * N : (z + 1) * N],
                 rhs=z_codes[z][:, b * P : (b + 1) * P].bitcast(FP8X4),
                 rhs_scale=z_scale[z][:, b * P : (b + 1) * P],
-                start=(z == 0),
-                stop=(z == 1),
+                start=(z == FRIENDS),
+                stop=(z == FOES),
             )
 
         held = room(2, "got0b", 2 * RAW_BYTES - OVERLAP)
@@ -279,32 +284,34 @@ def tile_picked_zsgn_mean_p_kernel(
         turned_sums(0, rooms0)
         held = room(2, "got1a", 0)
         rooms1 = (room(1, "f1") + held[:1] + room(1, "f12"), room(1, "e1") + held[1:] + room(1, "e12"))
-        rooms2, part = (room(3, "f2"), room(3, "e2")), (room(3, "f3"), room(3, "e3"))
+        rooms2, rooms3 = (room(3, "f2"), room(3, "e2")), (room(3, "f3"), room(3, "e3"))
         turned_sums(1, rooms1)
-        turned_sums(2, rooms2, range(5))
-        fetch(0, TURNED, 0, part[0])
-        turned_sums(2, rooms2, (5,))
+        last_step = 2 * DEGREE - 1
+        turned_sums(2, rooms2, range(last_step))
+        fetch(FRIENDS, DIRECT, 0, rooms3[FRIENDS])
+        turned_sums(2, rooms2, (last_step,))
 
-        def plane(z, first, width):
-            return z_grouped[z][:].rearrange("p (v j) -> p v j", j=PACK)[:, first : first + width, TURNED]
+        def direct_places(z, first, width):
+            return z_grouped[z][:].rearrange("p (v j) -> p v j", j=PACK)[:, first : first + width, DIRECT]
 
-        fetch(0, TURNED, 1, part[0])
-        fetch(1, TURNED, 0, part[1])
-        fetch(0, TURNED, 2, part[0])
-        nc.scalar.activation(plane(0, 0, V), part[0][2], ACT.Copy, scale=1.0 / DEGREE)
-        fetch(1, TURNED, 1, part[1], 0, P)
-        fetch(1, TURNED, 1, part[1], P, P)
-        fetch(1, TURNED, 2, part[1], 0, P)
-        nc.scalar.activation(plane(1, 0, P), part[1][2][:, :P], ACT.Copy, scale=1.0 / DEGREE)
-        fetch(1, TURNED, 2, part[1], P, P)
-        quantise_mean(0, 0, V)
-        nc.vector.tensor_scalar(plane(1, P, P), part[1][2][:, P:], 1.0 / DEGREE, None, ALU.mult)
+        fetch(FRIENDS, DIRECT, 1, rooms3[FRIENDS])
+        fetch(FOES, DIRECT, 0, rooms3[FOES])
+        fetch(FRIENDS, DIRECT, 2, rooms3[FRIENDS])
+        nc.scalar.activation(direct_places(FRIENDS, 0, V), rooms3[FRIENDS][2], ACT.Copy, scale=1.0 / DEGREE)
+        fetch(FOES, DIRECT, 1, rooms3[FOES], 0, P)
+        fetch(FOES, DIRECT, 1, rooms3[FOES], P, P)
+        fetch(FOES, DIRECT, 2, rooms3[FOES], 0, P)
+        nc.scalar.activation(direct_places(FOES, 0, P), rooms3[FOES][2][:, :P], ACT.Copy, scale=1.0 / DEGREE)
+        fetch(FOES, DIRECT, 2, rooms3[FOES], P, P)
+        quantise_mean(FRIENDS, 0, V)
+        nc.vector.tensor_scalar(direct_places(FOES, P, P), rooms3[FOES][2][:, P:], 1.0 / DEGREE, None, ALU.mult)
+
         acc = [psum.tile([P, P], F32, name=f"acc_out{b}", tag=f"bank{2 + b}") for b in range(HALVES)]
         for b in range(HALVES):
-            product(0, b, acc[b])
+            product(FRIENDS, b, acc[b])
         for b in range(HALVES):
-            quantise_mean(1, b * P, P)
-            product(1, b, acc[b])
+            quantise_mean(FOES, b * P, P)
+            product(FOES, b, acc[b])
             result = keep.tile([P, P], F32, name=f"result{b}", align_bytes=64)
             nc.scalar.activation(result[:], acc[b][:], ACT.Tanh)
             (nc.sync, nc.scalar)[b].dma_start(out[:, b * P : (b + 1) * P], result[:])

@@ -1,7 +1,6 @@
 from contextlib import ExitStack
 
 import concourse.mybir as mybir
-from concourse.masks import make_identity
 
 K, T, S, V, H, N = 1024, 1024, 512, 256, 512, 128
 FLOPS = 2 * K * H * S + 2 * 2 * H * N * V
@@ -21,19 +20,12 @@ P = 128
 PACK = 4
 K_PASS = P * PACK
 PASSES = K // K_PASS
-TILES = H // P
-HALVES = V // P
 DEGREE = 3
 LIST_ROWS = 16
 QUADRANT = 32
-DIRECT = TILES - 1
 FRIENDS, FOES = 0, 1
-PAIR_FIRST = (0, 43, 86, P)
-SINGLE_FIRST = (0, 42, 84, P)
-CHUNK_STEP, CHUNK_GROUPS = 42, 44
-RAW_BYTES = PACK * CHUNK_GROUPS * PACK * 4
-STAGE_COLS = 704
-OVERLAP = 64
+HALF = V // 2
+SCALAR_GROUPS = 22
 
 
 def tile_picked_zsgn_mean_p_kernel(
@@ -42,7 +34,6 @@ def tile_picked_zsgn_mean_p_kernel(
     nc = tc.nc
     with ExitStack() as ctx:
         keep = ctx.enter_context(tc.tile_pool(name="keep", bufs=1))
-        placed = ctx.enter_context(tc.tile_pool(name="placed", bufs=1))
         psum = ctx.enter_context(tc.psum_pool(name="psum", bufs=1))
 
         def load_list(src, name):
@@ -58,129 +49,30 @@ def tile_picked_zsgn_mean_p_kernel(
             nc.sync.dma_start(tile[:].bitcast(I32), x_words[o].rearrange("p n t -> p (n t)").bitcast(I32))
             return tile
 
-        def load_w1(c, o, offset=None):
-            shape = [P, PACK, CHUNK_GROUPS * PACK]
-            if offset is None:
-                tile = keep.tile(shape, F32, name=f"w1_raw{c}_{o}", tag=f"raw{c}_{o}", align_bytes=64)
-            else:
-                tile = placed.tile(shape, F32, name=f"w1_raw{c}_{o}", offset=offset, align_bytes=64)
-            first = c * CHUNK_STEP * PACK
-            width = max(PAIR_FIRST[c + 1], SINGLE_FIRST[c + 1]) * PACK - first
-            rows = w1[o * K_PASS : (o + 1) * K_PASS, first : first + width]
-            nc.sync.dma_start(tile[:, :, :width], rows.rearrange("(p j) c -> p j c", j=PACK))
+        def load_w1(o, g0, g1):
+            tile = keep.tile([P, PACK, (g1 - g0) * PACK], F32, name=f"w1_raw{o}_{g0}", align_bytes=64)
+            rows = w1[o * K_PASS : (o + 1) * K_PASS, g0 * PACK : g1 * PACK]
+            nc.sync.dma_start(tile[:], rows.rearrange("(p j) c -> p j c", j=PACK))
             return tile[:].rearrange("p j (m i) -> p m j i", i=PACK)
 
         scale_window = keep.tile([P, T], U8, name="scale_window", align_bytes=64)
         nc.gpsimd.memset(scale_window[:].bitcast(I32), 0)
         w_scales = keep.tile([P, 2 * N], U8, name="w_scales", align_bytes=64)
         nc.vector.memset(w_scales[:].bitcast(I32), 0)
-        ident = keep.tile([P, P], F32, name="ident", align_bytes=64)
-        make_identity(nc, ident[:])
 
         x_window = [load_words(0)]
         picked = load_list(offs, "offs")
         for q in range(P // QUADRANT):
             rows = slice(QUADRANT * q, QUADRANT * q + 4 * PASSES)
             nc.sync.dma_start(scale_window[rows, :].bitcast(I32), x_scales[:, 4 * q : 4 * q + 4, :].bitcast(I32))
-        w1_raw = {}
-        for o in range(PASSES):
-            w1_raw[0, o] = load_w1(0, o)
+        raw0 = [load_w1(0, 0, P // 2), load_w1(0, P // 2, P)]
         x_window.append(load_words(1))
-        w1_raw[1, 0] = load_w1(1, 0)
-        friends, foes = [load_list(pos1, "pos1")], [load_list(foe1, "foe1")]
-        w1_raw[1, 1] = load_w1(1, 1, RAW_BYTES)
-        friends.append(load_list(pos2, "pos2"))
-        foes.append(load_list(foe2, "foe2"))
-        friends.append(load_list(pos3, "pos3"))
-        foes.append(load_list(foe3, "foe3"))
-        w1_raw[2, 0] = load_w1(2, 0)
-        w1_raw[2, 1] = load_w1(2, 1, 0)
+        raw1 = [load_w1(1, 0, P // 2), load_w1(1, P // 2, P)]
+        friends, foes = [], []
+        for d, (p_src, q_src) in enumerate(((pos1, foe1), (pos2, foe2), (pos3, foe3))):
+            friends.append(load_list(p_src, f"pos{d}"))
+            foes.append(load_list(q_src, f"foe{d}"))
         lists = [friends, foes]
-
-        x_first = keep.tile([P, S], U32, name="x_codes0", align_bytes=64)
-        nc.vector.tensor_copy(x_first[:], x_window[0][:].indirect(picked[:]))
-        x_scale = keep.tile([P, S], U8, name="x_scale", align_bytes=64)
-        nc.vector.tensor_copy(x_scale[:], scale_window[:].indirect(picked[:]))
-
-        w1_codes, w1_scale = {}, {}
-
-        def cast_pairs(t, o):
-            g0, g1 = PAIR_FIRST[t], PAIR_FIRST[t + 1]
-            dst = stage[o][:, t * P : t * P + 2 * (g1 - g0), :].rearrange("p (m i) j -> p m j i", i=2)
-            nc.scalar.copy(dst, w1_raw[t, o][:, g0 - t * CHUNK_STEP : g1 - t * CHUNK_STEP, :, 0:2])
-
-        def cast_singles(t, o):
-            g0, g1 = SINGLE_FIRST[t], SINGLE_FIRST[t + 1]
-            first = (t + 1) * P - (g1 - g0)
-            apart = DIRECT * P + g0 - first
-            dst = stage[o][:, first : first + 2 * apart, :].rearrange("p (i m) j -> p m j i", i=2)[:, : g1 - g0]
-            src = w1_raw[t, o][:, : g1 - g0, :, 2:PACK]
-            if t > 0 and o == PASSES - 1:
-                for i in range(2):
-                    nc.scalar.copy(dst[:, :, :, i], src[:, :, :, i])
-            elif o == PASSES - 1:
-                nc.vector.tensor_copy(dst, src)
-            else:
-                nc.scalar.copy(dst, src)
-
-        def quantise_pass(t, o, scale_tag=None, tiles=1):
-            codes = keep.tile([P, tiles * P], U32, name=f"w1_codes{t}_{o}", align_bytes=64)
-            name = f"w1_scale{t}_{o}"
-            scale = keep.tile([P, tiles * P], U8, name=name, tag=scale_tag or name, align_bytes=64)
-            grouped = stage[o][:, t * P : (t + tiles) * P, :].rearrange("p c j -> p (c j)")
-            nc.vector.quantize_mx(out=codes[:].bitcast(FP8X4), scales=scale[:], in_=grouped)
-            for n in range(tiles):
-                w1_codes[t + n, o], w1_scale[t + n, o] = codes[:, n * P : (n + 1) * P], scale[:, n * P : (n + 1) * P]
-
-        def prepare_pass(t, o, scale_tag=None):
-            cast_pairs(t, o)
-            cast_singles(t, o)
-            quantise_pass(t, o, scale_tag)
-
-        stage = [keep.tile([P, STAGE_COLS, PACK], BF16, name=f"stage{o}", align_bytes=64) for o in range(PASSES)]
-        for o in range(PASSES):
-            prepare_pass(0, o)
-
-        pieces = ((0, 256), (256, 128), (384, 128))
-        x_late = [keep.tile([P, S // 2], U32, name=f"x_codes1_{s}", tag=f"raw0_{s}", align_bytes=64) for s in range(2)]
-
-        def picked_words(o, first, width):
-            if o == 0:
-                return x_first[:, first : first + width]
-            s, start = divmod(first, S // 2)
-            return x_late[s][:, start : start + width]
-
-        for first, width in pieces:
-            nc.vector.tensor_copy(picked_words(1, first, width), x_window[1][:].indirect(entries(picked, first, width)))
-
-        h = [keep.tile([P, S], F32, name=f"h{t}", align_bytes=64) for t in range(TILES)]
-
-        def hidden(t, first, width, tag, on_vector=False):
-            acc = psum.tile([P, width], F32, name=tag, tag=tag)
-            cols = slice(first, first + width)
-            group = min(width, S // 2)
-            for start in range(0, width, group):
-                for o in range(PASSES):
-                    nc.tensor.matmul_mx(
-                        out=acc[:, start : start + group],
-                        lhsT=w1_codes[t, o].bitcast(FP8X4),
-                        lhsT_scale=w1_scale[t, o],
-                        rhs=picked_words(o, first + start, group).bitcast(FP8X4),
-                        rhs_scale=x_scale[4 * o : P, first + start : first + start + group],
-                        start=(o == 0),
-                        stop=(o == PASSES - 1),
-                    )
-            if on_vector:
-                nc.vector.tensor_scalar(h[t][:, cols], acc[:], 0.0, None, ALU.max)
-            else:
-                nc.scalar.activation(h[t][:, cols], acc[:], ACT.Relu)
-
-        for (first, width), tag in zip(pieces, ("bank0", "bank1", "bank7")):
-            hidden(0, first, width, tag, on_vector=True)
-        prepare_pass(1, 0, scale_tag="w1_scale0_1")
-        prepare_pass(1, 1)
-        cast_pairs(2, 0)
-        cast_singles(2, 0)
         w_words = []
         for z, (words, scales) in enumerate(((w2_words, w2_scales), (w3_words, w3_scales))):
             tile = keep.tile([P, 2 * N], U8, name=f"w_words{z}", align_bytes=64)
@@ -191,127 +83,137 @@ def tile_picked_zsgn_mean_p_kernel(
                     w_scales[QUADRANT * q : QUADRANT * q + 4, z * N : (z + 1) * N].bitcast(I32),
                     scales[0, 4 * q : 4 * q + 4, :].bitcast(I32),
                 )
-        for s in range(2):
-            hidden(1, s * S // 2, S // 2, f"bank{6 + s}")
-        quantise_pass(2, 0, tiles=2)
-        prepare_pass(2, 1)
-        quantise_pass(DIRECT, 1)
-        for s in range(2):
-            hidden(2, s * S // 2, S // 2, f"bank{s}")
-        hidden(DIRECT, 0, S, "bank6")
 
-        mean_t = [keep.tile([P, HALVES, 2, P, 2], BF16, name=f"mean_t{z}", align_bytes=64) for z in range(2)]
+        x_codes = [keep.tile([P, S], U32, name="x_codes0", align_bytes=64)]
+        nc.vector.tensor_copy(x_codes[0][:], x_window[0][:].indirect(picked[:]))
+        x_scale = keep.tile([P, S], U8, name="x_scale", align_bytes=64)
+        nc.vector.tensor_copy(x_scale[:], scale_window[:].indirect(picked[:]))
 
-        def room(count, name, offset=None):
-            if offset is None:
-                tile = keep.tile([P, count, V], F32, name=name, align_bytes=64)
+        stage = [keep.tile([P, PACK, P, PACK], BF16, name=f"stage{o}", tag=f"stage{o}", align_bytes=64) for o in range(PASSES)]
+
+        def staged(o, g0, g1):
+            return stage[o][:, :, g0:g1, :].rearrange("p i m j -> p m j i")
+
+        w1_codes, w1_scale = {}, {}
+
+        def quantise_w1(o, t, tiles):
+            codes = keep.tile([P, tiles * P], U32, name=f"w1_codes{o}_{t}", align_bytes=64)
+            scale = keep.tile([P, tiles * P], U8, name=f"w1_scale{o}_{t}", align_bytes=64)
+            grouped = stage[o][:, t : t + tiles].rearrange("p i m j -> p (i m j)")
+            nc.vector.quantize_mx(out=codes[:].bitcast(FP8X4), scales=scale[:], in_=grouped)
+            for n in range(tiles):
+                w1_codes[o, t + n], w1_scale[o, t + n] = codes[:, n * P : (n + 1) * P], scale[:, n * P : (n + 1) * P]
+
+        def cast(o, half, raw, on_scalar):
+            first = half * P // 2
+            nc.scalar.copy(staged(o, first, first + on_scalar), raw[:, :on_scalar])
+            if on_scalar < P // 2:
+                nc.vector.tensor_copy(staged(o, first + on_scalar, first + P // 2), raw[:, on_scalar:])
+
+        cast(0, 0, raw0[0], P // 2)
+        cast(0, 1, raw0[1], SCALAR_GROUPS)
+        quantise_w1(0, 0, PACK)
+        x_codes.append(keep.tile([P, S], U32, name="x_codes1", tag="stage0", align_bytes=64))
+        nc.vector.tensor_copy(x_codes[1][:], x_window[1][:].indirect(picked[:]))
+        cast(1, 0, raw1[0], 40)
+        cast(1, 1, raw1[1], SCALAR_GROUPS)
+        quantise_w1(1, 0, 1)
+        quantise_w1(1, 1, 1)
+        quantise_w1(1, 2, 2)
+
+        h = [keep.tile([P, S], F32, name=f"h{t}", align_bytes=64) for t in range(PACK)]
+        pieces = [(0, 0, S // 2), (0, S // 2, S // 2), (1, 0, S), (2, 0, S), (3, 0, S)]
+        banks = [psum.tile([P, width], F32, name=f"bank{n}", tag=f"bank{n}") for n, (t, first, width) in enumerate(pieces)]
+        for o in range(PASSES):
+            for bank, (t, first, width) in zip(banks, pieces):
+                nc.tensor.matmul_mx(
+                    out=bank[:],
+                    lhsT=w1_codes[o, t].bitcast(FP8X4),
+                    lhsT_scale=w1_scale[o, t],
+                    rhs=x_codes[o][:, first : first + width].bitcast(FP8X4),
+                    rhs_scale=x_scale[4 * o : P, first : first + width],
+                    start=(o == 0),
+                    stop=(o == PASSES - 1),
+                )
+
+        def relu(n, on_vector):
+            t, first, width = pieces[n]
+            if on_vector:
+                nc.vector.tensor_scalar(h[t][:, first : first + width], banks[n][:], 0.0, 1.0 / DEGREE, ALU.max, ALU.mult)
             else:
-                tile = placed.tile([P, count, V], F32, name=name, offset=offset, align_bytes=64)
-            return [tile[:, i, :] for i in range(count)]
+                nc.scalar.activation(h[t][:, first : first + width], banks[n][:], ACT.Relu, scale=1.0 / DEGREE)
 
-        def fetch(z, t, d, rooms, first=0, width=V):
-            cols = slice(first, first + width)
-            window = h[t][:].indirect(entries(lists[z][d], first, width))
-            if d == 0:
-                nc.vector.tensor_copy(rooms[d][:, cols], window)
-            else:
-                nc.vector.tensor_tensor(rooms[d][:, cols], window, rooms[d - 1][:, cols], ALU.add)
+        rows = [[keep.tile([P, PACK, V], F32, name=f"rows{z}_{d}", align_bytes=64) for d in range(DEGREE)] for z in range(2)]
 
-        def turned_sums(t, rooms, steps=range(2 * DEGREE)):
-            for d, z in (divmod(step, 2) for step in steps):
-                fetch(z, t, d, rooms[z])
-                if d == DEGREE - 1:
-                    turn(z, t, rooms[z][d])
+        def fetch(z, t, d):
+            nc.scalar.activation(rows[z][d][:, t, :], h[t][:].indirect(lists[z][d][:]), ACT.Copy)
 
-        def round_turned(z, t, halves, bank):
-            g0, g1 = PAIR_FIRST[t], PAIR_FIRST[t + 1]
-            pairs = mean_t[z][:, halves, 0, g0:g1, :].rearrange("v b p e -> v b (p e)")
-            nc.scalar.activation(pairs, bank[:, :, : 2 * (g1 - g0)], ACT.Copy, scale=1.0 / DEGREE)
-            g0, g1 = SINGLE_FIRST[t], SINGLE_FIRST[t + 1]
-            singles = bank[:, :, P - (g1 - g0) :].unsqueeze(3).to_broadcast([P, bank.shape[1], g1 - g0, 2])
-            nc.scalar.activation(mean_t[z][:, halves, 1, g0:g1, :], singles, ACT.Copy, scale=1.0 / DEGREE)
+        def fetch_add(z, t, d, onto):
+            nc.vector.tensor_tensor(rows[z][d][:, t, :], h[t][:].indirect(lists[z][d][:]), rows[z][onto][:, t, :], ALU.add)
 
-        def turn(z, t, total):
-            if t < DIRECT - 1:
-                for b in range(HALVES):
-                    nc.tensor.transpose(sums[z][:, t, b, :], total[:, b * P : (b + 1) * P], ident[:])
-                if t == 1:
-                    for n in range(2):
-                        round_turned(z, n, slice(0, HALVES), sums[z][:, n])
-                return
-            banks = [psum.tile([P, 1, P], F32, name=f"late{z}_{b}", tag=f"bank{3 + 2 * z - b}") for b in range(HALVES)]
-            for b in range(HALVES):
-                nc.tensor.transpose(banks[b][:, 0, :], total[:, b * P : (b + 1) * P], ident[:])
-            for b in range(HALVES):
-                round_turned(z, t, slice(b, b + 1), banks[b][:])
-                turn_back(z, b)
+        z_grouped = [[keep.tile([P, HALF * PACK], BF16, name=f"z_grouped{z}_{b}", align_bytes=64) for b in range(2)] for z in range(2)]
+        z_codes = [[keep.tile([P, HALF], U32, name=f"z_codes{z}_{b}", align_bytes=64) for b in range(2)] for z in range(2)]
+        z_scale = [[keep.tile([P, HALF], U8, name=f"z_scale{z}_{b}", align_bytes=64) for b in range(2)] for z in range(2)]
 
-        sums = [psum.tile([P, 2, HALVES, P], F32, name=f"sum{z}", tag=f"bank{2 + 2 * z}") for z in range(2)]
-        z_grouped = [keep.tile([P, V * PACK], BF16, name=f"z_grouped{z}", align_bytes=64) for z in range(2)]
-        z_codes = [keep.tile([P, V], U32, name=f"z_codes{z}", align_bytes=64) for z in range(2)]
-        z_scale = [keep.tile([P, V], U8, name=f"z_scale{z}", align_bytes=64) for z in range(2)]
-        back_banks = (("bank0", "bank1"), ("bank6", "bank7"))
+        def grouped(z, b):
+            return z_grouped[z][b][:].rearrange("p (v e j) -> p v j e", e=2, j=PACK)
 
-        def turn_back(z, b):
-            words = mean_t[z][:, b].rearrange("v u p e -> v (u p e)").bitcast(F32)
-            back = psum.tile([P, 2, P], F32, name=f"back{z}_{b}", tag=back_banks[z][b])
-            for u in range(2):
-                nc.tensor.transpose(back[:, u, :], words[:, u * P : (u + 1) * P], ident[:])
-            half = z_grouped[z][:, b * P * PACK : (b + 1) * P * PACK]
-            nc.scalar.copy(half.bitcast(F32).rearrange("p (v u) -> p v u", u=2), back[:].rearrange("p u v -> p v u"))
+        def members(z, d, b):
+            return rows[z][d][:, :, b * HALF : (b + 1) * HALF].rearrange("p j (v e) -> p v j e", e=2)
 
-        def quantise_mean(z, first, width):
-            cols = slice(first, first + width)
-            nc.vector.quantize_mx(
-                out=z_codes[z][:, cols].bitcast(FP8X4),
-                scales=z_scale[z][:, cols],
-                in_=z_grouped[z][:, first * PACK : (first + width) * PACK],
-            )
+        def quantise_mean(z, b):
+            nc.vector.quantize_mx(out=z_codes[z][b][:].bitcast(FP8X4), scales=z_scale[z][b][:], in_=z_grouped[z][b][:])
 
         def product(z, b, acc):
             nc.tensor.matmul_mx(
                 out=acc[:],
                 lhsT=w_words[z][:].bitcast(FP4X4),
                 lhsT_scale=w_scales[:, z * N : (z + 1) * N],
-                rhs=z_codes[z][:, b * P : (b + 1) * P].bitcast(FP8X4),
-                rhs_scale=z_scale[z][:, b * P : (b + 1) * P],
-                start=(z == FRIENDS),
-                stop=(z == FOES),
+                rhs=z_codes[z][b][:].bitcast(FP8X4),
+                rhs_scale=z_scale[z][b][:],
+                start=(z == FOES),
+                stop=(z == FRIENDS),
             )
 
-        held = room(2, "got0b", 2 * RAW_BYTES - OVERLAP)
-        rooms0 = (room(1, "f0") + held[:1] + room(1, "f02"), room(1, "e0") + held[1:] + room(1, "e02"))
-        turned_sums(0, rooms0)
-        held = room(2, "got1a", 0)
-        rooms1 = (room(1, "f1") + held[:1] + room(1, "f12"), room(1, "e1") + held[1:] + room(1, "e12"))
-        rooms2, rooms3 = (room(3, "f2"), room(3, "e2")), (room(3, "f3"), room(3, "e3"))
-        turned_sums(1, rooms1)
-        last_step = 2 * DEGREE - 1
-        turned_sums(2, rooms2, range(last_step))
-        fetch(FRIENDS, DIRECT, 0, rooms3[FRIENDS])
-        turned_sums(2, rooms2, (last_step,))
+        relu(0, False)
+        relu(1, True)
+        relu(2, True)
+        fetch(FRIENDS, 0, 0)
+        fetch(FOES, 0, 0)
+        fetch(FRIENDS, 1, 0)
+        relu(3, False)
+        fetch(FOES, 1, 0)
+        fetch(FRIENDS, 2, 0)
+        relu(4, False)
+        fetch(FRIENDS, 3, 0)
+        fetch(FOES, 2, 0)
+        fetch(FRIENDS, 0, 1)
+        fetch(FOES, 3, 0)
+        for t in range(1, PACK):
+            fetch(FRIENDS, t, 1)
 
-        def direct_places(z, first, width):
-            return z_grouped[z][:].rearrange("p (v j) -> p v j", j=PACK)[:, first : first + width, DIRECT]
+        fetch_add(FRIENDS, 0, 2, 0)
+        fetch_add(FOES, 0, 1, 0)
+        fetch_add(FRIENDS, 1, 2, 0)
+        fetch_add(FOES, 0, 2, 1)
+        fetch_add(FOES, 1, 1, 0)
+        fetch_add(FRIENDS, 2, 2, 0)
+        fetch_add(FOES, 1, 2, 1)
+        fetch_add(FRIENDS, 3, 2, 0)
+        fetch_add(FOES, 2, 1, 0)
+        fetch_add(FOES, 3, 1, 0)
+        fetch_add(FOES, 2, 2, 1)
+        fetch_add(FOES, 3, 2, 1)
+        for b in range(2):
+            nc.scalar.copy(grouped(FOES, b), members(FOES, 2, b))
+        for b in range(2):
+            nc.vector.tensor_tensor(grouped(FRIENDS, b), members(FRIENDS, 1, b), members(FRIENDS, 2, b), ALU.add)
 
-        fetch(FRIENDS, DIRECT, 1, rooms3[FRIENDS])
-        fetch(FOES, DIRECT, 0, rooms3[FOES])
-        fetch(FRIENDS, DIRECT, 2, rooms3[FRIENDS])
-        nc.scalar.activation(direct_places(FRIENDS, 0, V), rooms3[FRIENDS][2], ACT.Copy, scale=1.0 / DEGREE)
-        fetch(FOES, DIRECT, 1, rooms3[FOES], 0, P)
-        fetch(FOES, DIRECT, 1, rooms3[FOES], P, P)
-        fetch(FOES, DIRECT, 2, rooms3[FOES], 0, P)
-        nc.scalar.activation(direct_places(FOES, 0, P), rooms3[FOES][2][:, :P], ACT.Copy, scale=1.0 / DEGREE)
-        fetch(FOES, DIRECT, 2, rooms3[FOES], P, P)
-        quantise_mean(FRIENDS, 0, V)
-        nc.vector.tensor_scalar(direct_places(FOES, P, P), rooms3[FOES][2][:, P:], 1.0 / DEGREE, None, ALU.mult)
-
-        acc = [psum.tile([P, P], F32, name=f"acc_out{b}", tag=f"bank{2 + b}") for b in range(HALVES)]
-        for b in range(HALVES):
-            product(FRIENDS, b, acc[b])
-        for b in range(HALVES):
-            quantise_mean(FOES, b * P, P)
-            product(FOES, b, acc[b])
-            result = keep.tile([P, P], F32, name=f"result{b}", align_bytes=64)
+        acc = [psum.tile([P, HALF], F32, name=f"acc_out{b}", tag=f"out{b}") for b in range(2)]
+        for b in range(2):
+            for z in (FOES, FRIENDS):
+                quantise_mean(z, b)
+                product(z, b, acc[b])
+            result = keep.tile([P, HALF], F32, name=f"result{b}", align_bytes=64)
             nc.scalar.activation(result[:], acc[b][:], ACT.Tanh)
-            (nc.sync, nc.scalar)[b].dma_start(out[:, b * P : (b + 1) * P], result[:])
+            (nc.sync, nc.scalar)[b].dma_start(out[:, b * HALF : (b + 1) * HALF], result[:])

@@ -25,7 +25,7 @@ LIST_ROWS = 16
 QUADRANT = 32
 FRIENDS, FOES = 0, 1
 HALF = V // 2
-SCALAR_GROUPS = 22
+SCALAR_GROUPS = 48
 
 
 def tile_picked_zsgn_mean_p_kernel(
@@ -65,9 +65,9 @@ def tile_picked_zsgn_mean_p_kernel(
         for q in range(P // QUADRANT):
             rows = slice(QUADRANT * q, QUADRANT * q + 4 * PASSES)
             nc.sync.dma_start(scale_window[rows, :].bitcast(I32), x_scales[:, 4 * q : 4 * q + 4, :].bitcast(I32))
-        raw0 = [load_w1(0, 0, P // 2), load_w1(0, P // 2, P)]
+        raw = [load_w1(0, 0, P)]
         x_window.append(load_words(1))
-        raw1 = [load_w1(1, 0, P // 2), load_w1(1, P // 2, P)]
+        raw.append(load_w1(1, 0, P))
         friends, foes = [], []
         for d, (p_src, q_src) in enumerate(((pos1, foe1), (pos2, foe2), (pos3, foe3))):
             friends.append(load_list(p_src, f"pos{d}"))
@@ -89,37 +89,40 @@ def tile_picked_zsgn_mean_p_kernel(
         x_scale = keep.tile([P, S], U8, name="x_scale", align_bytes=64)
         nc.vector.tensor_copy(x_scale[:], scale_window[:].indirect(picked[:]))
 
-        stage = [keep.tile([P, PACK, P, PACK], BF16, name=f"stage{o}", tag=f"stage{o}", align_bytes=64) for o in range(PASSES)]
-
-        def staged(o, g0, g1):
-            return stage[o][:, :, g0:g1, :].rearrange("p i m j -> p m j i")
-
+        stage = {
+            (o, u): keep.tile([P, 2, P, PACK], BF16, name=f"stage{o}_{u}", tag=f"stage{o}_{u}", align_bytes=64)
+            for o in range(PASSES)
+            for u in range(2)
+        }
         w1_codes, w1_scale = {}, {}
 
-        def quantise_w1(o, t, tiles):
-            codes = keep.tile([P, tiles * P], U32, name=f"w1_codes{o}_{t}", align_bytes=64)
-            scale = keep.tile([P, tiles * P], U8, name=f"w1_scale{o}_{t}", align_bytes=64)
-            grouped = stage[o][:, t : t + tiles].rearrange("p i m j -> p (i m j)")
+        def cast(o, u, g0, g1, on_vector):
+            dst = stage[o, u][:, :, g0:g1, :].rearrange("p e m j -> p m j e")
+            src = raw[o][:, g0:g1, :, 2 * u : 2 * u + 2]
+            if on_vector:
+                nc.vector.tensor_copy(dst, src)
+            else:
+                nc.scalar.copy(dst, src)
+
+        def quantise_w1(o, u):
+            codes = keep.tile([P, 2 * P], U32, name=f"w1_codes{o}_{u}", align_bytes=64)
+            scale = keep.tile([P, 2 * P], U8, name=f"w1_scale{o}_{u}", align_bytes=64)
+            grouped = stage[o, u][:].rearrange("p e m j -> p (e m j)")
             nc.vector.quantize_mx(out=codes[:].bitcast(FP8X4), scales=scale[:], in_=grouped)
-            for n in range(tiles):
-                w1_codes[o, t + n], w1_scale[o, t + n] = codes[:, n * P : (n + 1) * P], scale[:, n * P : (n + 1) * P]
+            for e in range(2):
+                w1_codes[o, 2 * u + e], w1_scale[o, 2 * u + e] = codes[:, e * P : (e + 1) * P], scale[:, e * P : (e + 1) * P]
 
-        def cast(o, half, raw, on_scalar):
-            first = half * P // 2
-            nc.scalar.copy(staged(o, first, first + on_scalar), raw[:, :on_scalar])
-            if on_scalar < P // 2:
-                nc.vector.tensor_copy(staged(o, first + on_scalar, first + P // 2), raw[:, on_scalar:])
-
-        cast(0, 0, raw0[0], P // 2)
-        cast(0, 1, raw0[1], SCALAR_GROUPS)
-        quantise_w1(0, 0, PACK)
-        x_codes.append(keep.tile([P, S], U32, name="x_codes1", tag="stage0", align_bytes=64))
+        cast(0, 0, 0, P, False)
+        cast(0, 1, 0, P, True)
+        quantise_w1(0, 1)
+        quantise_w1(0, 0)
+        x_codes.append(keep.tile([P, S], U32, name="x_codes1", tag="stage0_1", align_bytes=64))
         nc.vector.tensor_copy(x_codes[1][:], x_window[1][:].indirect(picked[:]))
-        cast(1, 0, raw1[0], 40)
-        cast(1, 1, raw1[1], SCALAR_GROUPS)
-        quantise_w1(1, 0, 1)
-        quantise_w1(1, 1, 1)
-        quantise_w1(1, 2, 2)
+        cast(1, 0, 0, SCALAR_GROUPS, False)
+        cast(1, 0, SCALAR_GROUPS, P, True)
+        quantise_w1(1, 0)
+        cast(1, 1, 0, P, False)
+        quantise_w1(1, 1)
 
         h = [keep.tile([P, S], F32, name=f"h{t}", align_bytes=64) for t in range(PACK)]
         pieces = [(0, 0, S // 2), (0, S // 2, S // 2), (1, 0, S), (2, 0, S), (3, 0, S)]

@@ -183,11 +183,13 @@ def tile_picked_zsgn_mean_p_kernel(
         relu(2, True)
         fetch(FRIENDS, 0, 0)
         fetch(FOES, 0, 0)
+        fetch_add(FRIENDS, 0, 2, 0)
+        fetch_add(FOES, 0, 1, 0)
+        relu(4, True)
         fetch(FRIENDS, 1, 0)
         relu(3, False)
         fetch(FOES, 1, 0)
         fetch(FRIENDS, 2, 0)
-        relu(4, False)
         fetch(FRIENDS, 3, 0)
         fetch(FOES, 2, 0)
         fetch(FRIENDS, 0, 1)
@@ -195,8 +197,6 @@ def tile_picked_zsgn_mean_p_kernel(
         for t in range(1, PACK):
             fetch(FRIENDS, t, 1)
 
-        fetch_add(FRIENDS, 0, 2, 0)
-        fetch_add(FOES, 0, 1, 0)
         fetch_add(FRIENDS, 1, 2, 0)
         fetch_add(FOES, 0, 2, 1)
         fetch_add(FOES, 1, 1, 0)

@@ -125,7 +125,7 @@ def tile_picked_zsgn_mean_p_kernel(
         quantise_w1(1, 1)
 
         h = [keep.tile([P, S], F32, name=f"h{t}", align_bytes=64) for t in range(PACK)]
-        pieces = [(0, 0, S // 2), (0, S // 2, S // 2), (1, 0, S), (2, 0, S), (3, 0, S)]
+        pieces = [(0, 0, S // 2), (0, S // 2, S // 2), (1, 0, S), (2, 0, S), (3, 0, S // 2), (3, S // 2, S // 2)]
         banks = [psum.tile([P, width], F32, name=f"bank{n}", tag=f"bank{n}") for n, (t, first, width) in enumerate(pieces)]
         for o in range(PASSES):
             for bank, (t, first, width) in zip(banks, pieces):
@@ -185,27 +185,27 @@ def tile_picked_zsgn_mean_p_kernel(
         fetch(FOES, 0, 0)
         fetch_add(FRIENDS, 0, 2, 0)
         fetch_add(FOES, 0, 1, 0)
-        relu(4, True)
         fetch(FRIENDS, 1, 0)
+        fetch_add(FRIENDS, 1, 2, 0)
+        relu(5, True)
         relu(3, False)
         fetch(FOES, 1, 0)
         fetch(FRIENDS, 2, 0)
-        fetch(FRIENDS, 3, 0)
+        relu(4, False)
         fetch(FOES, 2, 0)
-        fetch(FRIENDS, 0, 1)
         fetch(FOES, 3, 0)
-        for t in range(1, PACK):
+        fetch(FRIENDS, 3, 0)
+        for t in range(PACK):
             fetch(FRIENDS, t, 1)
 
-        fetch_add(FRIENDS, 1, 2, 0)
         fetch_add(FOES, 0, 2, 1)
         fetch_add(FOES, 1, 1, 0)
         fetch_add(FRIENDS, 2, 2, 0)
         fetch_add(FOES, 1, 2, 1)
-        fetch_add(FRIENDS, 3, 2, 0)
         fetch_add(FOES, 2, 1, 0)
         fetch_add(FOES, 3, 1, 0)
         fetch_add(FOES, 2, 2, 1)
+        fetch_add(FRIENDS, 3, 2, 0)
         fetch_add(FOES, 3, 2, 1)
         for b in range(2):
             nc.scalar.copy(grouped(FOES, b), members(FOES, 2, b))

@@ -25,7 +25,7 @@ LIST_ROWS = 16
 QUADRANT = 32
 FRIENDS, FOES = 0, 1
 HALF = V // 2
-SCALAR_GROUPS = 48
+SCALAR_GROUPS = 40
 
 
 def tile_picked_zsgn_mean_p_kernel(
@@ -49,14 +49,14 @@ def tile_picked_zsgn_mean_p_kernel(
             nc.sync.dma_start(tile[:].bitcast(I32), x_words[o].rearrange("p n t -> p (n t)").bitcast(I32))
             return tile
 
-        def load_w1(o, g0, g1):
-            tile = keep.tile([P, PACK, (g1 - g0) * PACK], F32, name=f"w1_raw{o}_{g0}", align_bytes=64)
-            rows = w1[o * K_PASS : (o + 1) * K_PASS, g0 * PACK : g1 * PACK]
-            nc.sync.dma_start(tile[:], rows.rearrange("(p j) c -> p j c", j=PACK))
+        def load_w1(o, j0, j1):
+            tile = keep.tile([P, j1 - j0, H], F32, name=f"w1_raw{o}_{j0}", align_bytes=64)
+            rows = w1[o * K_PASS : (o + 1) * K_PASS, :]
+            nc.sync.dma_start(tile[:], rows.rearrange("(p j) c -> p j c", j=PACK)[:, j0:j1])
             return tile[:].rearrange("p j (m i) -> p m j i", i=PACK)
 
         scale_window = keep.tile([P, T], U8, name="scale_window", align_bytes=64)
-        nc.gpsimd.memset(scale_window[:].bitcast(I32), 0)
+        nc.vector.memset(scale_window[:].bitcast(I32), 0)
         w_scales = keep.tile([P, 2 * N], U8, name="w_scales", align_bytes=64)
         nc.vector.memset(w_scales[:].bitcast(I32), 0)
 
@@ -65,9 +65,9 @@ def tile_picked_zsgn_mean_p_kernel(
         for q in range(P // QUADRANT):
             rows = slice(QUADRANT * q, QUADRANT * q + 4 * PASSES)
             nc.sync.dma_start(scale_window[rows, :].bitcast(I32), x_scales[:, 4 * q : 4 * q + 4, :].bitcast(I32))
-        raw = [load_w1(0, 0, P)]
+        raw = {(0, 0): load_w1(0, 0, PACK)}
         x_window.append(load_words(1))
-        raw.append(load_w1(1, 0, P))
+        raw[1, 0], raw[1, 2] = load_w1(1, 0, 2), load_w1(1, 2, PACK)
         friends, foes = [], []
         for d, (p_src, q_src) in enumerate(((pos1, foe1), (pos2, foe2), (pos3, foe3))):
             friends.append(load_list(p_src, f"pos{d}"))
@@ -96,21 +96,21 @@ def tile_picked_zsgn_mean_p_kernel(
         }
         w1_codes, w1_scale = {}, {}
 
-        def cast(o, u, g0, g1, on_vector):
-            dst = stage[o, u][:, :, g0:g1, :].rearrange("p e m j -> p m j e")
-            src = raw[o][:, g0:g1, :, 2 * u : 2 * u + 2]
+        def cast(o, u, g0, g1, on_vector, j0=0):
+            src = raw[o, j0][:, g0:g1, :, 2 * u : 2 * u + 2]
+            dst = stage[o, u][:, :, g0:g1, j0 : j0 + src.shape[2]].rearrange("p e m j -> p m j e")
             if on_vector:
                 nc.vector.tensor_copy(dst, src)
             else:
                 nc.scalar.copy(dst, src)
 
-        def quantise_w1(o, u):
-            codes = keep.tile([P, 2 * P], U32, name=f"w1_codes{o}_{u}", align_bytes=64)
-            scale = keep.tile([P, 2 * P], U8, name=f"w1_scale{o}_{u}", align_bytes=64)
-            grouped = stage[o, u][:].rearrange("p e m j -> p (e m j)")
+        def quantise_w1(o, u, e0=0, e1=2):
+            codes = keep.tile([P, (e1 - e0) * P], U32, name=f"w1_codes{o}_{u}_{e0}", align_bytes=64)
+            scale = keep.tile([P, (e1 - e0) * P], U8, name=f"w1_scale{o}_{u}_{e0}", align_bytes=64)
+            grouped = stage[o, u][:, e0:e1].rearrange("p e m j -> p (e m j)")
             nc.vector.quantize_mx(out=codes[:].bitcast(FP8X4), scales=scale[:], in_=grouped)
-            for e in range(2):
-                w1_codes[o, 2 * u + e], w1_scale[o, 2 * u + e] = codes[:, e * P : (e + 1) * P], scale[:, e * P : (e + 1) * P]
+            for n, e in enumerate(range(e0, e1)):
+                w1_codes[o, 2 * u + e], w1_scale[o, 2 * u + e] = codes[:, n * P : (n + 1) * P], scale[:, n * P : (n + 1) * P]
 
         cast(0, 0, 0, P, False)
         cast(0, 1, 0, P, True)
@@ -118,10 +118,13 @@ def tile_picked_zsgn_mean_p_kernel(
         quantise_w1(0, 0)
         x_codes.append(keep.tile([P, S], U32, name="x_codes1", tag="stage0_1", align_bytes=64))
         nc.vector.tensor_copy(x_codes[1][:], x_window[1][:].indirect(picked[:]))
-        cast(1, 0, 0, SCALAR_GROUPS, False)
-        cast(1, 0, SCALAR_GROUPS, P, True)
-        quantise_w1(1, 0)
-        cast(1, 1, 0, P, False)
+        cast(1, 0, 0, P, False)
+        cast(1, 1, 0, P, True)
+        cast(1, 0, 0, SCALAR_GROUPS, False, 2)
+        cast(1, 0, SCALAR_GROUPS, P, True, 2)
+        quantise_w1(1, 0, 0, 1)
+        quantise_w1(1, 0, 1, 2)
+        cast(1, 1, 0, P, False, 2)
         quantise_w1(1, 1)
 
         h = [keep.tile([P, S], F32, name=f"h{t}", align_bytes=64) for t in range(PACK)]

@@ -25,7 +25,7 @@ LIST_ROWS = 16
 QUADRANT = 32
 FRIENDS, FOES = 0, 1
 HALF = V // 2
-SCALAR_GROUPS = 40
+SCALAR_GROUPS = 48
 
 
 def tile_picked_zsgn_mean_p_kernel(
@@ -49,10 +49,10 @@ def tile_picked_zsgn_mean_p_kernel(
             nc.sync.dma_start(tile[:].bitcast(I32), x_words[o].rearrange("p n t -> p (n t)").bitcast(I32))
             return tile
 
-        def load_w1(o, j0, j1):
-            tile = keep.tile([P, j1 - j0, H], F32, name=f"w1_raw{o}_{j0}", align_bytes=64)
+        def load_w1(o):
+            tile = keep.tile([P, PACK, H], F32, name=f"w1_raw{o}", align_bytes=64)
             rows = w1[o * K_PASS : (o + 1) * K_PASS, :]
-            nc.sync.dma_start(tile[:], rows.rearrange("(p j) c -> p j c", j=PACK)[:, j0:j1])
+            nc.sync.dma_start(tile[:], rows.rearrange("(p j) c -> p j c", j=PACK))
             return tile[:].rearrange("p j (m i) -> p m j i", i=PACK)
 
         scale_window = keep.tile([P, T], U8, name="scale_window", align_bytes=64)
@@ -62,12 +62,18 @@ def tile_picked_zsgn_mean_p_kernel(
 
         x_window = [load_words(0)]
         picked = load_list(offs, "offs")
-        for q in range(P // QUADRANT):
-            rows = slice(QUADRANT * q, QUADRANT * q + 4 * PASSES)
-            nc.sync.dma_start(scale_window[rows, :].bitcast(I32), x_scales[:, 4 * q : 4 * q + 4, :].bitcast(I32))
-        raw = {(0, 0): load_w1(0, 0, PACK)}
+
+
+        def load_scales(o):
+            for q in range(P // QUADRANT):
+                rows = slice(QUADRANT * q + 4 * o, QUADRANT * q + 4 * o + 4)
+                nc.sync.dma_start(scale_window[rows, :].bitcast(I32), x_scales[o, 4 * q : 4 * q + 4, :].bitcast(I32))
+
+        load_scales(0)
+        raw = [load_w1(0)]
+        load_scales(1)
         x_window.append(load_words(1))
-        raw[1, 0], raw[1, 2] = load_w1(1, 0, 2), load_w1(1, 2, PACK)
+        raw.append(load_w1(1))
         friends, foes = [], []
         for d, (p_src, q_src) in enumerate(((pos1, foe1), (pos2, foe2), (pos3, foe3))):
             friends.append(load_list(p_src, f"pos{d}"))
@@ -96,9 +102,9 @@ def tile_picked_zsgn_mean_p_kernel(
         }
         w1_codes, w1_scale = {}, {}
 
-        def cast(o, u, g0, g1, on_vector, j0=0):
-            src = raw[o, j0][:, g0:g1, :, 2 * u : 2 * u + 2]
-            dst = stage[o, u][:, :, g0:g1, j0 : j0 + src.shape[2]].rearrange("p e m j -> p m j e")
+        def cast(o, u, g0, g1, on_vector):
+            src = raw[o][:, g0:g1, :, 2 * u : 2 * u + 2]
+            dst = stage[o, u][:, :, g0:g1, :].rearrange("p e m j -> p m j e")
             if on_vector:
                 nc.vector.tensor_copy(dst, src)
             else:
@@ -113,18 +119,16 @@ def tile_picked_zsgn_mean_p_kernel(
                 w1_codes[o, 2 * u + e], w1_scale[o, 2 * u + e] = codes[:, n * P : (n + 1) * P], scale[:, n * P : (n + 1) * P]
 
         cast(0, 0, 0, P, False)
-        cast(0, 1, 0, P, True)
-        quantise_w1(0, 1)
+        cast(0, 1, 0, P, False)
         quantise_w1(0, 0)
-        x_codes.append(keep.tile([P, S], U32, name="x_codes1", tag="stage0_1", align_bytes=64))
+        x_codes.append(keep.tile([P, S], U32, name="x_codes1", align_bytes=64))
         nc.vector.tensor_copy(x_codes[1][:], x_window[1][:].indirect(picked[:]))
-        cast(1, 0, 0, P, False)
-        cast(1, 1, 0, P, True)
-        cast(1, 0, 0, SCALAR_GROUPS, False, 2)
-        cast(1, 0, SCALAR_GROUPS, P, True, 2)
+        quantise_w1(0, 1)
+        cast(1, 0, 0, SCALAR_GROUPS, False)
+        cast(1, 0, SCALAR_GROUPS, P, True)
         quantise_w1(1, 0, 0, 1)
         quantise_w1(1, 0, 1, 2)
-        cast(1, 1, 0, P, False, 2)
+        cast(1, 1, 0, P, False)
         quantise_w1(1, 1)
 
         h = [keep.tile([P, S], F32, name=f"h{t}", align_bytes=64) for t in range(PACK)]
@@ -157,26 +161,31 @@ def tile_picked_zsgn_mean_p_kernel(
         def fetch_add(z, t, d, onto):
             nc.vector.tensor_tensor(rows[z][d][:, t, :], h[t][:].indirect(lists[z][d][:]), rows[z][onto][:, t, :], ALU.add)
 
-        z_grouped = [[keep.tile([P, HALF * PACK], BF16, name=f"z_grouped{z}_{b}", align_bytes=64) for b in range(2)] for z in range(2)]
-        z_codes = [[keep.tile([P, HALF], U32, name=f"z_codes{z}_{b}", align_bytes=64) for b in range(2)] for z in range(2)]
-        z_scale = [[keep.tile([P, HALF], U8, name=f"z_scale{z}_{b}", align_bytes=64) for b in range(2)] for z in range(2)]
+        z_grouped = [keep.tile([P, 2 * HALF * PACK], BF16, name=f"z_grouped{b}", align_bytes=64) for b in range(2)]
+        z_codes = [keep.tile([P, 2 * HALF], U32, name=f"z_codes{b}", align_bytes=64) for b in range(2)]
+        z_scale = [keep.tile([P, 2 * HALF], U8, name=f"z_scale{b}", align_bytes=64) for b in range(2)]
 
         def grouped(z, b):
-            return z_grouped[z][b][:].rearrange("p (v e j) -> p v j e", e=2, j=PACK)
+            return z_grouped[b][:, z * HALF * PACK : (z + 1) * HALF * PACK].rearrange("p (v e j) -> p v j e", e=2, j=PACK)
 
         def members(z, d, b):
             return rows[z][d][:, :, b * HALF : (b + 1) * HALF].rearrange("p j (v e) -> p v j e", e=2)
 
-        def quantise_mean(z, b):
-            nc.vector.quantize_mx(out=z_codes[z][b][:].bitcast(FP8X4), scales=z_scale[z][b][:], in_=z_grouped[z][b][:])
+        def quantise_means(b, z0, z1):
+            cols = slice(z0 * HALF, z1 * HALF)
+            nc.vector.quantize_mx(
+                out=z_codes[b][:, cols].bitcast(FP8X4),
+                scales=z_scale[b][:, cols],
+                in_=z_grouped[b][:, z0 * HALF * PACK : z1 * HALF * PACK],
+            )
 
         def product(z, b, acc):
             nc.tensor.matmul_mx(
                 out=acc[:],
                 lhsT=w_words[z][:].bitcast(FP4X4),
                 lhsT_scale=w_scales[:, z * N : (z + 1) * N],
-                rhs=z_codes[z][b][:].bitcast(FP8X4),
-                rhs_scale=z_scale[z][b][:],
+                rhs=z_codes[b][:, z * HALF : (z + 1) * HALF].bitcast(FP8X4),
+                rhs_scale=z_scale[b][:, z * HALF : (z + 1) * HALF],
                 start=(z == FOES),
                 stop=(z == FRIENDS),
             )
@@ -217,9 +226,10 @@ def tile_picked_zsgn_mean_p_kernel(
 
         acc = [psum.tile([P, HALF], F32, name=f"acc_out{b}", tag=f"out{b}") for b in range(2)]
         for b in range(2):
-            for z in (FOES, FRIENDS):
-                quantise_mean(z, b)
-                product(z, b, acc[b])
+            for z0, z1 in (((FRIENDS, FOES + 1),), ((FOES, FOES + 1), (FRIENDS, FOES)))[b]:
+                quantise_means(b, z0, z1)
+                for z in reversed(range(z0, z1)):
+                    product(z, b, acc[b])
             result = keep.tile([P, HALF], F32, name=f"result{b}", align_bytes=64)
             nc.scalar.activation(result[:], acc[b][:], ACT.Tanh)
             (nc.sync, nc.scalar)[b].dma_start(out[:, b * HALF : (b + 1) * HALF], result[:])

@@ -45,7 +45,7 @@ def tile_picked_zsgn_mean_p_kernel(
             return list_tile[:, first // LIST_ROWS : (first + width) // LIST_ROWS]
 
         def load_words(o):
-            tile = keep.tile([P, T], U32, name=f"x_window{o}", align_bytes=64)
+            tile = keep.tile([P, T], U32, name=f"x_window{o}", tag=f"x_window{o}", align_bytes=64)
             nc.sync.dma_start(tile[:].bitcast(I32), x_words[o].rearrange("p n t -> p (n t)").bitcast(I32))
             return tile
 
@@ -72,13 +72,11 @@ def tile_picked_zsgn_mean_p_kernel(
         load_scales(0)
         raw = [load_w1(0)]
         load_scales(1)
-        x_window.append(load_words(1))
         raw.append(load_w1(1))
-        friends, foes = [], []
-        for d, (p_src, q_src) in enumerate(((pos1, foe1), (pos2, foe2), (pos3, foe3))):
-            friends.append(load_list(p_src, f"pos{d}"))
-            foes.append(load_list(q_src, f"foe{d}"))
-        lists = [friends, foes]
+        lists = [{0: load_list(pos1, "pos1")}, {0: load_list(foe1, "foe1")}]
+        lists[FRIENDS][2], lists[FOES][1] = load_list(pos3, "pos3"), load_list(foe2, "foe2")
+        x_window.append(load_words(1))
+        lists[FOES][2], lists[FRIENDS][1] = load_list(foe3, "foe3"), load_list(pos2, "pos2")
         w_words = []
         for z, (words, scales) in enumerate(((w2_words, w2_scales), (w3_words, w3_scales))):
             tile = keep.tile([P, 2 * N], U8, name=f"w_words{z}", align_bytes=64)
@@ -110,8 +108,9 @@ def tile_picked_zsgn_mean_p_kernel(
             else:
                 nc.scalar.copy(dst, src)
 
-        def quantise_w1(o, u, e0=0, e1=2):
-            codes = keep.tile([P, (e1 - e0) * P], U32, name=f"w1_codes{o}_{u}_{e0}", align_bytes=64)
+        def quantise_w1(o, u, e0=0, e1=2, tag=None):
+            name = f"w1_codes{o}_{u}_{e0}"
+            codes = keep.tile([P, (e1 - e0) * P], U32, name=name, tag=tag or name, align_bytes=64)
             scale = keep.tile([P, (e1 - e0) * P], U8, name=f"w1_scale{o}_{u}_{e0}", align_bytes=64)
             grouped = stage[o, u][:, e0:e1].rearrange("p e m j -> p (e m j)")
             nc.vector.quantize_mx(out=codes[:].bitcast(FP8X4), scales=scale[:], in_=grouped)
@@ -119,20 +118,21 @@ def tile_picked_zsgn_mean_p_kernel(
                 w1_codes[o, 2 * u + e], w1_scale[o, 2 * u + e] = codes[:, n * P : (n + 1) * P], scale[:, n * P : (n + 1) * P]
 
         cast(0, 0, 0, P, False)
-        cast(0, 1, 0, P, False)
+        cast(0, 1, 0, P // 2, False)
+        cast(0, 1, P // 2, P, True)
         quantise_w1(0, 0)
-        x_codes.append(keep.tile([P, S], U32, name="x_codes1", align_bytes=64))
-        nc.vector.tensor_copy(x_codes[1][:], x_window[1][:].indirect(picked[:]))
         quantise_w1(0, 1)
         cast(1, 0, 0, SCALAR_GROUPS, False)
         cast(1, 0, SCALAR_GROUPS, P, True)
-        quantise_w1(1, 0, 0, 1)
-        quantise_w1(1, 0, 1, 2)
+        quantise_w1(1, 0)
         cast(1, 1, 0, P, False)
-        quantise_w1(1, 1)
+        x_codes.append(keep.tile([P, S], U32, name="x_codes1", tag="stage1_0", align_bytes=64))
+        for first, width in ((0, 256), (256, 128), (384, 128)):
+            nc.vector.tensor_copy(x_codes[1][:, first : first + width], x_window[1][:].indirect(entries(picked, first, width)))
+        quantise_w1(1, 1, tag="x_window1")
 
-        h = [keep.tile([P, S], F32, name=f"h{t}", align_bytes=64) for t in range(PACK)]
-        pieces = [(0, 0, S // 2), (0, S // 2, S // 2), (1, 0, S), (2, 0, S), (3, 0, S // 2), (3, S // 2, S // 2)]
+        h = {t: keep.tile([P, S], F32, name=f"h{t}", align_bytes=64) for t in (0, 1, 3)}
+        pieces = [(0, 0, 256), (1, 0, 256), (0, 256, 128), (0, 384, 128), (1, 256, 256), (3, 0, S), (2, 0, S)]
         banks = [psum.tile([P, width], F32, name=f"bank{n}", tag=f"bank{n}") for n, (t, first, width) in enumerate(pieces)]
         for o in range(PASSES):
             for bank, (t, first, width) in zip(banks, pieces):
@@ -155,11 +155,16 @@ def tile_picked_zsgn_mean_p_kernel(
 
         rows = [[keep.tile([P, PACK, V], F32, name=f"rows{z}_{d}", align_bytes=64) for d in range(DEGREE)] for z in range(2)]
 
+        lead = keep.tile([P, V], F32, name="lead", tag="lead", align_bytes=64)
+
+        def row(z, d, t):
+            return lead[:] if (z, d, t) == (FRIENDS, 0, 0) else rows[z][d][:, t, :]
+
         def fetch(z, t, d):
-            nc.scalar.activation(rows[z][d][:, t, :], h[t][:].indirect(lists[z][d][:]), ACT.Copy)
+            nc.scalar.activation(row(z, d, t), h[t][:].indirect(lists[z][d][:]), ACT.Copy)
 
         def fetch_add(z, t, d, onto):
-            nc.vector.tensor_tensor(rows[z][d][:, t, :], h[t][:].indirect(lists[z][d][:]), rows[z][onto][:, t, :], ALU.add)
+            nc.vector.tensor_tensor(rows[z][d][:, t, :], h[t][:].indirect(lists[z][d][:]), row(z, onto, t), ALU.add)
 
         z_grouped = [keep.tile([P, 2 * HALF * PACK], BF16, name=f"z_grouped{b}", align_bytes=64) for b in range(2)]
         z_codes = [keep.tile([P, 2 * HALF], U32, name=f"z_codes{b}", align_bytes=64) for b in range(2)]
@@ -186,24 +191,26 @@ def tile_picked_zsgn_mean_p_kernel(
                 lhsT_scale=w_scales[:, z * N : (z + 1) * N],
                 rhs=z_codes[b][:, z * HALF : (z + 1) * HALF].bitcast(FP8X4),
                 rhs_scale=z_scale[b][:, z * HALF : (z + 1) * HALF],
-                start=(z == FOES),
-                stop=(z == FRIENDS),
+                start=(z == FRIENDS),
+                stop=(z == FOES),
             )
 
         relu(0, False)
+        relu(2, False)
+        relu(3, False)
         relu(1, True)
-        relu(2, True)
+        relu(4, True)
+        relu(5, True)
         fetch(FRIENDS, 0, 0)
         fetch(FOES, 0, 0)
         fetch_add(FRIENDS, 0, 2, 0)
         fetch_add(FOES, 0, 1, 0)
         fetch(FRIENDS, 1, 0)
         fetch_add(FRIENDS, 1, 2, 0)
-        relu(5, True)
-        relu(3, False)
+        h[2] = keep.tile([P, S], F32, name="h2", tag="lead", align_bytes=64)
+        relu(6, False)
         fetch(FOES, 1, 0)
         fetch(FRIENDS, 2, 0)
-        relu(4, False)
         fetch(FOES, 2, 0)
         fetch(FOES, 3, 0)
         fetch(FRIENDS, 3, 0)
@@ -224,11 +231,11 @@ def tile_picked_zsgn_mean_p_kernel(
         for b in range(2):
             nc.vector.tensor_tensor(grouped(FRIENDS, b), members(FRIENDS, 1, b), members(FRIENDS, 2, b), ALU.add)
 
-        acc = [psum.tile([P, HALF], F32, name=f"acc_out{b}", tag=f"out{b}") for b in range(2)]
+        acc = [psum.tile([P, HALF], F32, name=f"acc_out{b}", tag=f"bank{2 + b}") for b in range(2)]
         for b in range(2):
-            for z0, z1 in (((FRIENDS, FOES + 1),), ((FOES, FOES + 1), (FRIENDS, FOES)))[b]:
+            for z0, z1 in (((FRIENDS, FOES + 1),), ((FRIENDS, FOES), (FOES, FOES + 1)))[b]:
                 quantise_means(b, z0, z1)
-                for z in reversed(range(z0, z1)):
+                for z in range(z0, z1):
                     product(z, b, acc[b])
             result = keep.tile([P, HALF], F32, name=f"result{b}", align_bytes=64)
             nc.scalar.activation(result[:], acc[b][:], ACT.Tanh)

@@ -25,7 +25,7 @@ LIST_ROWS = 16
 QUADRANT = 32
 FRIENDS, FOES = 0, 1
 HALF = V // 2
-SCALAR_GROUPS = 48
+SCALAR_GROUPS = 56
 
 
 def tile_picked_zsgn_mean_p_kernel(
@@ -73,9 +73,9 @@ def tile_picked_zsgn_mean_p_kernel(
         raw = [load_w1(0)]
         load_scales(1)
         raw.append(load_w1(1))
+        x_window.append(load_words(1))
         lists = [{0: load_list(pos1, "pos1")}, {0: load_list(foe1, "foe1")}]
         lists[FRIENDS][2], lists[FOES][1] = load_list(pos3, "pos3"), load_list(foe2, "foe2")
-        x_window.append(load_words(1))
         lists[FOES][2], lists[FRIENDS][1] = load_list(foe3, "foe3"), load_list(pos2, "pos2")
         w_words = []
         for z, (words, scales) in enumerate(((w2_words, w2_scales), (w3_words, w3_scales))):
@@ -94,7 +94,7 @@ def tile_picked_zsgn_mean_p_kernel(
         nc.vector.tensor_copy(x_scale[:], scale_window[:].indirect(picked[:]))
 
         stage = {
-            (o, u): keep.tile([P, 2, P, PACK], BF16, name=f"stage{o}_{u}", tag=f"stage{o}_{u}", align_bytes=64)
+            (o, u): keep.tile([P, 2, P, PACK], BF16, name=f"stage{o}_{u}", align_bytes=64)
             for o in range(PASSES)
             for u in range(2)
         }
@@ -126,25 +126,32 @@ def tile_picked_zsgn_mean_p_kernel(
         cast(1, 0, SCALAR_GROUPS, P, True)
         quantise_w1(1, 0)
         cast(1, 1, 0, P, False)
-        x_codes.append(keep.tile([P, S], U32, name="x_codes1", tag="stage1_0", align_bytes=64))
+        x_codes.append(keep.tile([P, S], U32, name="x_codes1", align_bytes=64))
         for first, width in ((0, 256), (256, 128), (384, 128)):
             nc.vector.tensor_copy(x_codes[1][:, first : first + width], x_window[1][:].indirect(entries(picked, first, width)))
         quantise_w1(1, 1, tag="x_window1")
 
         h = {t: keep.tile([P, S], F32, name=f"h{t}", align_bytes=64) for t in (0, 1, 3)}
-        pieces = [(0, 0, 256), (1, 0, 256), (0, 256, 128), (0, 384, 128), (1, 256, 256), (3, 0, S), (2, 0, S)]
-        banks = [psum.tile([P, width], F32, name=f"bank{n}", tag=f"bank{n}") for n, (t, first, width) in enumerate(pieces)]
+        pieces = [(0, 0, 256), (1, 0, 256), (0, 256, 128), (0, 384, 128), (1, 256, 256), (3, 0, 256), (2, 0, S), (3, 256, 256)]
+        banks = {}
+
+        def multiply(n, o, tag):
+            t, first, width = pieces[n]
+            if o == 0:
+                banks[n] = psum.tile([P, width], F32, name=f"piece{n}", tag=tag)
+            nc.tensor.matmul_mx(
+                out=banks[n][:],
+                lhsT=w1_codes[o, t].bitcast(FP8X4),
+                lhsT_scale=w1_scale[o, t],
+                rhs=x_codes[o][:, first : first + width].bitcast(FP8X4),
+                rhs_scale=x_scale[4 * o : P, first : first + width],
+                start=(o == 0),
+                stop=(o == PASSES - 1),
+            )
+
         for o in range(PASSES):
-            for bank, (t, first, width) in zip(banks, pieces):
-                nc.tensor.matmul_mx(
-                    out=bank[:],
-                    lhsT=w1_codes[o, t].bitcast(FP8X4),
-                    lhsT_scale=w1_scale[o, t],
-                    rhs=x_codes[o][:, first : first + width].bitcast(FP8X4),
-                    rhs_scale=x_scale[4 * o : P, first : first + width],
-                    start=(o == 0),
-                    stop=(o == PASSES - 1),
-                )
+            for n in range(len(pieces) - 1):
+                multiply(n, o, f"bank{n}")
 
         def relu(n, on_vector):
             t, first, width = pieces[n]
@@ -160,8 +167,9 @@ def tile_picked_zsgn_mean_p_kernel(
         def row(z, d, t):
             return lead[:] if (z, d, t) == (FRIENDS, 0, 0) else rows[z][d][:, t, :]
 
-        def fetch(z, t, d):
-            nc.scalar.activation(row(z, d, t), h[t][:].indirect(lists[z][d][:]), ACT.Copy)
+        def fetch(z, t, d, first=0, width=V):
+            window = h[t][:].indirect(entries(lists[z][d], first, width))
+            nc.scalar.activation(row(z, d, t)[:, first : first + width], window, ACT.Copy)
 
         def fetch_add(z, t, d, onto):
             nc.vector.tensor_tensor(rows[z][d][:, t, :], h[t][:].indirect(lists[z][d][:]), row(z, onto, t), ALU.add)
@@ -196,11 +204,13 @@ def tile_picked_zsgn_mean_p_kernel(
             )
 
         relu(0, False)
+        relu(1, False)
         relu(2, False)
         relu(3, False)
-        relu(1, True)
         relu(4, True)
         relu(5, True)
+        for o in range(PASSES):
+            multiply(7, o, "bank3")
         fetch(FRIENDS, 0, 0)
         fetch(FOES, 0, 0)
         fetch_add(FRIENDS, 0, 2, 0)
@@ -211,11 +221,14 @@ def tile_picked_zsgn_mean_p_kernel(
         relu(6, False)
         fetch(FOES, 1, 0)
         fetch(FRIENDS, 2, 0)
+        relu(7, False)
         fetch(FOES, 2, 0)
         fetch(FOES, 3, 0)
         fetch(FRIENDS, 3, 0)
-        for t in range(PACK):
+        for t in range(PACK - 1):
             fetch(FRIENDS, t, 1)
+        for b in range(2):
+            fetch(FRIENDS, PACK - 1, 1, b * HALF, HALF)
 
         fetch_add(FOES, 0, 2, 1)
         fetch_add(FOES, 1, 1, 0)
@@ -231,7 +244,7 @@ def tile_picked_zsgn_mean_p_kernel(
         for b in range(2):
             nc.vector.tensor_tensor(grouped(FRIENDS, b), members(FRIENDS, 1, b), members(FRIENDS, 2, b), ALU.add)
 
-        acc = [psum.tile([P, HALF], F32, name=f"acc_out{b}", tag=f"bank{2 + b}") for b in range(2)]
+        acc = [psum.tile([P, HALF], F32, name=f"acc_out{b}", tag=f"bank{b}") for b in range(2)]
         for b in range(2):
             for z0, z1 in (((FRIENDS, FOES + 1),), ((FRIENDS, FOES), (FOES, FOES + 1)))[b]:
                 quantise_means(b, z0, z1)

from contextlib import ExitStack

import concourse.mybir as mybir

K, T, S, V, H, N = 1024, 1024, 512, 256, 512, 128
FLOPS = 2 * K * H * S + 2 * 2 * H * N * V

F32 = mybir.dt.float32
BF16 = mybir.dt.bfloat16
I32 = mybir.dt.int32
U32 = mybir.dt.uint32
U16 = mybir.dt.uint16
U8 = mybir.dt.uint8
FP8X4 = mybir.dt.float8_e4m3fn_x4
FP4X4 = mybir.dt.float4_e2m1fn_x4
ACT = mybir.ActivationFunctionType
ALU = mybir.AluOpType

P = 128
PACK = 4
K_PASS = P * PACK
PASSES = K // K_PASS
DEGREE = 3
LIST_ROWS = 16
QUADRANT = 32
FRIENDS, FOES = 0, 1
HALF = V // 2
SCALAR_GROUPS = 56


def tile_picked_zsgn_mean_p_kernel(
    tc, x_words, x_scales, w1, w2_words, w2_scales, w3_words, w3_scales, offs, pos1, pos2, pos3, foe1, foe2, foe3, out
):
    nc = tc.nc
    with ExitStack() as ctx:
        keep = ctx.enter_context(tc.tile_pool(name="keep", bufs=1))
        psum = ctx.enter_context(tc.psum_pool(name="psum", bufs=1))

        def load_list(src, name):
            tile = keep.tile(list(src.shape), U16, name=name)
            nc.sync.dma_start(tile[:], src)
            return tile

        def entries(list_tile, first, width):
            return list_tile[:, first // LIST_ROWS : (first + width) // LIST_ROWS]

        def load_words(o):
            tile = keep.tile([P, T], U32, name=f"x_window{o}", tag=f"x_window{o}", align_bytes=64)
            nc.sync.dma_start(tile[:].bitcast(I32), x_words[o].rearrange("p n t -> p (n t)").bitcast(I32))
            return tile

        def load_w1(o):
            tile = keep.tile([P, PACK, H], F32, name=f"w1_raw{o}", align_bytes=64)
            rows = w1[o * K_PASS : (o + 1) * K_PASS, :]
            nc.sync.dma_start(tile[:], rows.rearrange("(p j) c -> p j c", j=PACK))
            return tile[:].rearrange("p j (m i) -> p m j i", i=PACK)

        scale_window = keep.tile([P, T], U8, name="scale_window", align_bytes=64)
        nc.vector.memset(scale_window[:].bitcast(I32), 0)
        w_scales = keep.tile([P, 2 * N], U8, name="w_scales", align_bytes=64)
        nc.vector.memset(w_scales[:].bitcast(I32), 0)

        x_window = [load_words(0)]
        picked = load_list(offs, "offs")


        def load_scales(o):
            for q in range(P // QUADRANT):
                rows = slice(QUADRANT * q + 4 * o, QUADRANT * q + 4 * o + 4)
                nc.sync.dma_start(scale_window[rows, :].bitcast(I32), x_scales[o, 4 * q : 4 * q + 4, :].bitcast(I32))

        load_scales(0)
        raw = [load_w1(0)]
        load_scales(1)
        raw.append(load_w1(1))
        x_window.append(load_words(1))
        lists = [{0: load_list(pos1, "pos1")}, {0: load_list(foe1, "foe1")}]
        lists[FRIENDS][2], lists[FOES][1] = load_list(pos3, "pos3"), load_list(foe2, "foe2")
        lists[FOES][2], lists[FRIENDS][1] = load_list(foe3, "foe3"), load_list(pos2, "pos2")
        w_words = []
        for z, (words, scales) in enumerate(((w2_words, w2_scales), (w3_words, w3_scales))):
            tile = keep.tile([P, 2 * N], U8, name=f"w_words{z}", align_bytes=64)
            nc.sync.dma_start(tile[:].bitcast(I32), words[0].bitcast(I32))
            w_words.append(tile)
            for q in range(P // QUADRANT):
                nc.sync.dma_start(
                    w_scales[QUADRANT * q : QUADRANT * q + 4, z * N : (z + 1) * N].bitcast(I32),
                    scales[0, 4 * q : 4 * q + 4, :].bitcast(I32),
                )

        x_codes = [keep.tile([P, S], U32, name="x_codes0", align_bytes=64)]
        nc.vector.tensor_copy(x_codes[0][:], x_window[0][:].indirect(picked[:]))
        x_scale = keep.tile([P, S], U8, name="x_scale", align_bytes=64)
        nc.vector.tensor_copy(x_scale[:], scale_window[:].indirect(picked[:]))

        stage = {
            (o, u): keep.tile([P, 2, P, PACK], BF16, name=f"stage{o}_{u}", align_bytes=64)
            for o in range(PASSES)
            for u in range(2)
        }
        w1_codes, w1_scale = {}, {}

        def cast(o, u, g0, g1, on_vector):
            src = raw[o][:, g0:g1, :, 2 * u : 2 * u + 2]
            dst = stage[o, u][:, :, g0:g1, :].rearrange("p e m j -> p m j e")
            if on_vector:
                nc.vector.tensor_copy(dst, src)
            else:
                nc.scalar.copy(dst, src)

        def quantise_w1(o, u, e0=0, e1=2, tag=None):
            name = f"w1_codes{o}_{u}_{e0}"
            codes = keep.tile([P, (e1 - e0) * P], U32, name=name, tag=tag or name, align_bytes=64)
            scale = keep.tile([P, (e1 - e0) * P], U8, name=f"w1_scale{o}_{u}_{e0}", align_bytes=64)
            grouped = stage[o, u][:, e0:e1].rearrange("p e m j -> p (e m j)")
            nc.vector.quantize_mx(out=codes[:].bitcast(FP8X4), scales=scale[:], in_=grouped)
            for n, e in enumerate(range(e0, e1)):
                w1_codes[o, 2 * u + e], w1_scale[o, 2 * u + e] = codes[:, n * P : (n + 1) * P], scale[:, n * P : (n + 1) * P]

        cast(0, 0, 0, P, False)
        cast(0, 1, 0, P // 2, False)
        cast(0, 1, P // 2, P, True)
        quantise_w1(0, 0)
        quantise_w1(0, 1)
        cast(1, 0, 0, SCALAR_GROUPS, False)
        cast(1, 0, SCALAR_GROUPS, P, True)
        quantise_w1(1, 0)
        cast(1, 1, 0, P, False)
        x_codes.append(keep.tile([P, S], U32, name="x_codes1", align_bytes=64))
        for first, width in ((0, 256), (256, 128), (384, 128)):
            nc.vector.tensor_copy(x_codes[1][:, first : first + width], x_window[1][:].indirect(entries(picked, first, width)))
        quantise_w1(1, 1, tag="x_window1")

        h = {t: keep.tile([P, S], F32, name=f"h{t}", align_bytes=64) for t in (0, 1, 3)}
        pieces = [(0, 0, 256), (1, 0, 256), (0, 256, 128), (0, 384, 128), (1, 256, 256), (3, 0, 256), (2, 0, S), (3, 256, 256)]
        banks = {}

        def multiply(n, o, tag):
            t, first, width = pieces[n]
            if o == 0:
                banks[n] = psum.tile([P, width], F32, name=f"piece{n}", tag=tag)
            nc.tensor.matmul_mx(
                out=banks[n][:],
                lhsT=w1_codes[o, t].bitcast(FP8X4),
                lhsT_scale=w1_scale[o, t],
                rhs=x_codes[o][:, first : first + width].bitcast(FP8X4),
                rhs_scale=x_scale[4 * o : P, first : first + width],
                start=(o == 0),
                stop=(o == PASSES - 1),
            )

        for o in range(PASSES):
            for n in range(len(pieces) - 1):
                multiply(n, o, f"bank{n}")

        def relu(n, on_vector):
            t, first, width = pieces[n]
            if on_vector:
                nc.vector.tensor_scalar(h[t][:, first : first + width], banks[n][:], 0.0, 1.0 / DEGREE, ALU.max, ALU.mult)
            else:
                nc.scalar.activation(h[t][:, first : first + width], banks[n][:], ACT.Relu, scale=1.0 / DEGREE)

        rows = [[keep.tile([P, PACK, V], F32, name=f"rows{z}_{d}", align_bytes=64) for d in range(DEGREE)] for z in range(2)]

        lead = keep.tile([P, V], F32, name="lead", tag="lead", align_bytes=64)

        def row(z, d, t):
            return lead[:] if (z, d, t) == (FRIENDS, 0, 0) else rows[z][d][:, t, :]

        def fetch(z, t, d, first=0, width=V):
            window = h[t][:].indirect(entries(lists[z][d], first, width))
            nc.scalar.activation(row(z, d, t)[:, first : first + width], window, ACT.Copy)

        def fetch_add(z, t, d, onto):
            nc.vector.tensor_tensor(rows[z][d][:, t, :], h[t][:].indirect(lists[z][d][:]), row(z, onto, t), ALU.add)

        z_grouped = [keep.tile([P, 2 * HALF * PACK], BF16, name=f"z_grouped{b}", align_bytes=64) for b in range(2)]
        z_codes = [keep.tile([P, 2 * HALF], U32, name=f"z_codes{b}", align_bytes=64) for b in range(2)]
        z_scale = [keep.tile([P, 2 * HALF], U8, name=f"z_scale{b}", align_bytes=64) for b in range(2)]

        def grouped(z, b):
            return z_grouped[b][:, z * HALF * PACK : (z + 1) * HALF * PACK].rearrange("p (v e j) -> p v j e", e=2, j=PACK)

        def members(z, d, b):
            return rows[z][d][:, :, b * HALF : (b + 1) * HALF].rearrange("p j (v e) -> p v j e", e=2)

        def quantise_means(b, z0, z1):
            cols = slice(z0 * HALF, z1 * HALF)
            nc.vector.quantize_mx(
                out=z_codes[b][:, cols].bitcast(FP8X4),
                scales=z_scale[b][:, cols],
                in_=z_grouped[b][:, z0 * HALF * PACK : z1 * HALF * PACK],
            )

        def product(z, b, acc):
            nc.tensor.matmul_mx(
                out=acc[:],
                lhsT=w_words[z][:].bitcast(FP4X4),
                lhsT_scale=w_scales[:, z * N : (z + 1) * N],
                rhs=z_codes[b][:, z * HALF : (z + 1) * HALF].bitcast(FP8X4),
                rhs_scale=z_scale[b][:, z * HALF : (z + 1) * HALF],
                start=(z == FRIENDS),
                stop=(z == FOES),
            )

        relu(0, False)
        relu(1, False)
        relu(2, False)
        relu(3, False)
        relu(4, True)
        relu(5, True)
        for o in range(PASSES):
            multiply(7, o, "bank3")
        fetch(FRIENDS, 0, 0)
        fetch(FOES, 0, 0)
        fetch_add(FRIENDS, 0, 2, 0)
        fetch_add(FOES, 0, 1, 0)
        fetch(FRIENDS, 1, 0)
        fetch_add(FRIENDS, 1, 2, 0)
        h[2] = keep.tile([P, S], F32, name="h2", tag="lead", align_bytes=64)
        relu(6, False)
        fetch(FOES, 1, 0)
        fetch(FRIENDS, 2, 0)
        relu(7, False)
        fetch(FOES, 2, 0)
        fetch(FOES, 3, 0)
        fetch(FRIENDS, 3, 0)
        for t in range(PACK - 1):
            fetch(FRIENDS, t, 1)
        for b in range(2):
            fetch(FRIENDS, PACK - 1, 1, b * HALF, HALF)

        fetch_add(FOES, 0, 2, 1)
        fetch_add(FOES, 1, 1, 0)
        fetch_add(FRIENDS, 2, 2, 0)
        fetch_add(FOES, 1, 2, 1)
        fetch_add(FOES, 2, 1, 0)
        fetch_add(FOES, 3, 1, 0)
        fetch_add(FOES, 2, 2, 1)
        fetch_add(FRIENDS, 3, 2, 0)
        fetch_add(FOES, 3, 2, 1)
        for b in range(2):
            nc.scalar.copy(grouped(FOES, b), members(FOES, 2, b))
        for b in range(2):
            nc.vector.tensor_tensor(grouped(FRIENDS, b), members(FRIENDS, 1, b), members(FRIENDS, 2, b), ALU.add)

        acc = [psum.tile([P, HALF], F32, name=f"acc_out{b}", tag=f"bank{b}") for b in range(2)]
        for b in range(2):
            for z0, z1 in (((FRIENDS, FOES + 1),), ((FRIENDS, FOES), (FOES, FOES + 1)))[b]:
                quantise_means(b, z0, z1)
                for z in range(z0, z1):
                    product(z, b, acc[b])
            result = keep.tile([P, HALF], F32, name=f"result{b}", align_bytes=64)
            nc.scalar.activation(result[:], acc[b][:], ACT.Tanh)
            (nc.sync, nc.scalar)[b].dma_start(out[:, b * HALF : (b + 1) * HALF], result[:])
